import numpy as np
import ml_dtypes


def mxq(x, axis, fmt="e4m3"):
    dtype, down = {"e4m3": (ml_dtypes.float8_e4m3fn, 7), "e5m2": (ml_dtypes.float8_e5m2, 14)}[fmt]
    v = np.moveaxis(np.asarray(x, np.float32).astype(ml_dtypes.bfloat16).astype(np.float64), axis, -1)
    blocks = v.reshape(v.shape[:-1] + (-1, 32))
    amax = np.abs(blocks).max(-1, keepdims=True)
    byte = np.maximum(np.where(amax > 0, np.frexp(amax)[1] - 1 + 127, 0) - down, 1)
    scale = np.exp2(byte - 127.0)
    codes = (blocks / scale).astype(np.float32).astype(dtype).astype(np.float64)
    return np.moveaxis((codes * scale).reshape(v.shape), -1, axis)


WIDE = False


def mx_kscale(k):
    if not WIDE:
        return np.ones(k)
    levels = np.array([10, -10, 5, -5, 0])
    if k % 512:
        return np.exp2(np.random.permutation(np.resize(levels, k // 32))).repeat(32)
    a = np.empty((k // 512, 16))
    for p in range(k // 512):
        a[p, :8] = np.random.permutation(np.resize(levels, 8))
        for g in range(8):
            far = levels[np.abs(levels - a[p, g]) >= 10]
            a[p, g + 8] = far[np.random.randint(len(far))]
    return np.exp2(a.ravel()).repeat(32)


def f64(x):
    return np.asarray(x).astype(np.float64)


def striped8(idx):
    return np.concatenate([x.reshape(-1, 16).T for x in idx]).astype(np.uint16)


def runs(offs, k):
    lists = np.stack([offs[16 * r : 16 * r + 16].T.reshape(-1) for r in range(8)]).astype(np.int64)
    return lists[np.arange(k) % 512 // 64]


def pack_weight(w):
    k, n = w.shape
    w = f64(np.asarray(w, np.float32).astype(ml_dtypes.bfloat16)).reshape(k // 32, 32, n)
    amax = np.abs(w).max(1)
    byte = np.clip(np.where(amax > 0, np.frexp(amax)[1] - 1 + 127 - 7, 1), 1, 254)
    scaled = (w * np.exp2(127.0 - byte)[:, None, :]).reshape(k, n).astype(np.float32)
    words = np.ascontiguousarray(scaled.reshape(k // 512, 128, 4, n).transpose(0, 1, 3, 2)).astype(ml_dtypes.float8_e4m3fn).view(np.uint8)
    return words, np.ascontiguousarray(byte.astype(np.uint8).reshape(k // 512, 16, n))


def unpack_weight(words, scales):
    g, p, n, _ = words.shape
    vals = np.ascontiguousarray(words).view(ml_dtypes.float8_e4m3fn).astype(np.float64) * np.repeat(np.exp2(scales.astype(np.float64) - 127.0), 8, axis=1)[..., None]
    return vals.transpose(0, 1, 3, 2).reshape(g * 512, n)


E2M1 = np.array([0.0, 0.5, 1.0, 1.5, 2.0, 3.0, 4.0, 6.0, -0.0, -0.5, -1.0, -1.5, -2.0, -3.0, -4.0, -6.0])


def pack_fp4(w):
    k, n = w.shape
    w = f64(np.asarray(w, np.float32).astype(ml_dtypes.bfloat16)).reshape(k // 32, 32, n)
    amax = np.abs(w).max(1)
    mant, ex = np.frexp(amax / 6.0)
    byte = np.clip(np.where(amax > 0, np.where(mant > 0.5, ex, ex - 1) + 127, 1), 1, 254)
    scaled = (w * np.exp2(127.0 - byte)[:, None, :]).reshape(k, n).astype(np.float32)
    c = np.ascontiguousarray(scaled.reshape(k // 512, 128, 4, n).transpose(0, 1, 3, 2)).astype(ml_dtypes.float4_e2m1fn).view(np.uint8) & 0xF
    words = (c[..., 0::2] | (c[..., 1::2] << 4)).reshape(k // 512, 128, 2 * n)
    return np.ascontiguousarray(words), np.ascontiguousarray(byte.astype(np.uint8).reshape(k // 512, 16, n))


def unpack_fp4(words, scales):
    g, _, n = scales.shape
    words = np.ascontiguousarray(words).reshape(g, 128, n, 2)
    nib = np.empty((g, 128, n, 4), np.uint8)
    nib[..., 0::2] = words & 0xF
    nib[..., 1::2] = words >> 4
    vals = E2M1[nib] * np.repeat(np.exp2(scales.astype(np.float64) - 127.0), 8, axis=1)[..., None]
    return vals.transpose(0, 1, 3, 2).reshape(g * 512, n)


def relu(v):
    return np.maximum(v, 0.0)


K, T, S, H, N = 512, 2048, 1024, 512, 256


def setup_inputs():
    n = np.random.standard_normal
    s = mx_kscale(K)[:, None]
    u = mx_kscale(H)
    packed_xT = pack_weight(n((K, T)) * s)
    packed_w2 = pack_fp4(n((H, N)) / np.sqrt(H) / u[:, None])
    return {
        "x_words": packed_xT[0],
        "x_scales": packed_xT[1],
        "w1": (n((K, H)) / np.sqrt(K) / s * u).astype(np.float32),
        "w2_words": packed_w2[0],
        "w2_scales": packed_w2[1],
        "offs": striped8(np.stack([np.random.permutation(T)[:S] for _ in range(8)])),
    }


def reference(x_words, x_scales, w1, w2_words, w2_scales, offs):
    xq = unpack_weight(x_words, x_scales)[np.arange(K)[:, None], runs(offs, K)]
    h = relu(mxq(f64(w1), 0, "e4m3").T @ xq)
    return unpack_fp4(w2_words, w2_scales).T @ mxq(h, 0, "e4m3")

@@ -1,0 +1,144 @@
+from contextlib import ExitStack
+
+import concourse.mybir as mybir
+
+K, T, S, H, N = 512, 2048, 1024, 512, 256
+FLOPS = 2 * K * H * S + 2 * H * N * S
+
+F32 = mybir.dt.float32
+BF16 = mybir.dt.bfloat16
+I32 = mybir.dt.int32
+U32 = mybir.dt.uint32
+U16 = mybir.dt.uint16
+U8 = mybir.dt.uint8
+FP8X4 = mybir.dt.float8_e4m3fn_x4
+FP4X4 = mybir.dt.float4_e2m1fn_x4
+RELU = mybir.ActivationFunctionType.Relu
+
+P = 128
+PACK = 4
+UNIT = 256
+CHUNK = 128
+VECTOR_RELU = (3, 5)
+
+
+def tile_picked_phmlp_relu_p_kernel(tc, x_words, x_scales, w1, w2_words, w2_scales, offs, out):
+    nc = tc.nc
+    with ExitStack() as ctx:
+        keep = ctx.enter_context(tc.tile_pool(name="keep", bufs=1))
+        psum = ctx.enter_context(tc.psum_pool(name="psum", bufs=8))
+
+        offsets = keep.tile([P, S // 16], U16, name="offsets")
+        nc.sync.dma_start(offsets[:], offs)
+
+        xs_table = keep.tile([P, T], U8, name="xs_table", align_bytes=64)
+        nc.vector.memset(xs_table[:].bitcast(I32), 0)
+        nc.scalar.dma_start(xs_table[0:P:8, :].bitcast(I32), x_scales[0].bitcast(I32))
+
+        w1_rows = w1.rearrange("(p j) c -> p j c", j=PACK)
+        w1_raw = []
+        for u in range(2):
+            raw = keep.tile([P, PACK, H // 2], F32, name=f"w1_raw{u}")
+            nc.sync.dma_start(raw[:], w1_rows[:, :, u * (H // 2) : (u + 1) * (H // 2)])
+            w1_raw.append(raw)
+
+        xw_table = keep.tile([P, T], U32, name="xw_table", align_bytes=64)
+        nc.sync.dma_start(xw_table[:].bitcast(I32), x_words[0].rearrange("p n t -> p (n t)").bitcast(I32))
+
+        w2_codes = keep.tile([P, 2 * N], U8, name="w2_codes", align_bytes=64)
+        nc.sync.dma_start(w2_codes[:].bitcast(I32), w2_words[0].bitcast(I32))
+        w2_plane = keep.tile([P, N], U8, name="w2_plane", align_bytes=64)
+        nc.gpsimd.memset(w2_plane[:].bitcast(I32), 0)
+        for q in range(4):
+            nc.gpsimd.dma_start(w2_plane[32 * q : 32 * q + 4, :].bitcast(I32), w2_scales[0, 4 * q : 4 * q + 4, :].bitcast(I32))
+
+        xs_plane = keep.tile([P, S], U8, name="xs_plane", align_bytes=64)
+        nc.vector.memset(xs_plane[:].bitcast(I32), 0)
+        xs_picked = keep.tile([P, S], U8, name="xs_picked", align_bytes=64)
+        nc.vector.tensor_copy(xs_picked[:], xs_table[:].indirect(offsets[:]))
+        for r in range(4):
+            nc.sync.dma_start(xs_plane[r:P:32, :].bitcast(I32), xs_picked[8 * r : P : 32, :].bitcast(I32))
+
+        w1_bf = keep.tile([P, PACK, P, PACK], BF16, name="w1_bf", align_bytes=64)
+        for u in range(2):
+            dst = w1_bf[:, :, 64 * u : 64 * (u + 1), :].rearrange("p t m j -> p m t j")
+            src = w1_raw[u][:].rearrange("p j (m t) -> p m t j", t=PACK)
+            if u == 0:
+                nc.scalar.copy(dst, src)
+            else:
+                nc.scalar.copy(dst[:, 0:24], src[:, 0:24])
+                nc.vector.tensor_copy(dst[:, 24:64], src[:, 24:64])
+        w1_codes = keep.tile([P, H], U32, name="w1_codes", align_bytes=64)
+        w1_plane = keep.tile([P, H], U8, name="w1_plane", align_bytes=64)
+        nc.vector.quantize_mx(out=w1_codes[:].bitcast(FP8X4), scales=w1_plane[:], in_=w1_bf[:].rearrange("p t m j -> p (t m j)"))
+
+        xw_picked = []
+        for u in range(S // UNIT):
+            g = keep.tile([P, UNIT], U32, name=f"xw_picked{u}", align_bytes=64)
+            nc.vector.tensor_copy(g[:], xw_table[:].indirect(offsets[:, u * (UNIT // 16) : (u + 1) * (UNIT // 16)]))
+            xw_picked.append(g)
+
+        out_rows = out.rearrange("(a p) s -> p a s", p=P)
+
+        h_bf = [keep.tile([P, UNIT, PACK], BF16, name=f"h_bf{u}", align_bytes=64) for u in range(S // UNIT)]
+
+        def first_layer(c):
+            u, e = divmod(c, UNIT // CHUNK)
+            bank = psum.tile([P, PACK, CHUNK], F32, name="h_bank", tag="bank")
+            for t in range(PACK):
+                nc.tensor.matmul_mx(
+                    out=bank[:, t, :],
+                    lhsT=w1_codes[:, t * P : (t + 1) * P].bitcast(FP8X4),
+                    lhsT_scale=w1_plane[:, t * P : (t + 1) * P],
+                    rhs=xw_picked[u][:, e * CHUNK : (e + 1) * CHUNK].bitcast(FP8X4),
+                    rhs_scale=xs_plane[:, c * CHUNK : (c + 1) * CHUNK],
+                    start=True,
+                    stop=True,
+                )
+            dst = h_bf[u][:, e * CHUNK : (e + 1) * CHUNK, :]
+            src = bank[:].rearrange("p t n -> p n t")
+            if c in VECTOR_RELU:
+                nc.vector.tensor_scalar_max(dst, src, 0.0)
+            else:
+                nc.scalar.activation(dst, src, RELU)
+
+        def quantise_hidden(u):
+            h_codes = keep.tile([P, UNIT], U32, name=f"h_codes{u}", align_bytes=64)
+            h_plane = keep.tile([P, UNIT], U8, name=f"h_plane{u}", align_bytes=64)
+            nc.vector.quantize_mx(out=h_codes[:].bitcast(FP8X4), scales=h_plane[:], in_=h_bf[u][:].rearrange("p n t -> p (n t)"))
+            return h_codes, h_plane
+
+        def second_pass(dst, a, h_codes, h_plane):
+            nc.tensor.matmul_mx(
+                out=dst,
+                lhsT=w2_codes[:, a * 2 * P : (a + 1) * 2 * P].bitcast(FP4X4),
+                lhsT_scale=w2_plane[:, a * P : (a + 1) * P],
+                rhs=h_codes[:].bitcast(FP8X4),
+                rhs_scale=h_plane[:],
+                start=True,
+                stop=True,
+            )
+
+        for c in range(S // CHUNK):
+            first_layer(c)
+        last = S // UNIT - 1
+        for u in range(S // UNIT):
+            h_codes, h_plane = quantise_hidden(u)
+            res = keep.tile([P, N // P, UNIT], F32, name=f"res{u}")
+            if u < last:
+                bank = psum.tile([P, N // P, UNIT], F32, name="o_bank", tag="bank")
+                for a in range(N // P):
+                    second_pass(bank[:, a, :], a, h_codes, h_plane)
+                if u == 1:
+                    nc.vector.tensor_copy(res[:], bank[:])
+                else:
+                    nc.scalar.copy(res[:], bank[:])
+            else:
+                for a in range(N // P):
+                    bank = psum.tile([P, UNIT], F32, name="o_half", tag="bank")
+                    second_pass(bank[:], a, h_codes, h_plane)
+                    if a == 0:
+                        nc.vector.tensor_copy(res[:, a, :], bank[:])
+                    else:
+                        nc.scalar.copy(res[:, a, :], bank[:])
+            nc.sync.dma_start(out_rows[:, :, u * UNIT : (u + 1) * UNIT], res[:])

@@ -18,8 +18,12 @@ RELU = mybir.ActivationFunctionType.Relu
 P = 128
 PACK = 4
 UNIT = 256
+HALF = 512
 CHUNK = 128
-VECTOR_RELU = (3, 5)
+VECTOR_RELU = (2, 4)
+ZERO_SPLIT = 1280
+WARM = 1
+W1_PIECES = ((0, 128), (128, 256), (256, 512))
 
 
 def tile_picked_phmlp_relu_p_kernel(tc, x_words, x_scales, w1, w2_words, w2_scales, offs, out):
@@ -28,49 +32,58 @@ def tile_picked_phmlp_relu_p_kernel(tc, x_words, x_scales, w1, w2_words, w2_scal
         keep = ctx.enter_context(tc.tile_pool(name="keep", bufs=1))
         psum = ctx.enter_context(tc.psum_pool(name="psum", bufs=8))
 
-        offsets = keep.tile([P, S // 16], U16, name="offsets")
-        nc.sync.dma_start(offsets[:], offs)
-
         xs_table = keep.tile([P, T], U8, name="xs_table", align_bytes=64)
-        nc.vector.memset(xs_table[:].bitcast(I32), 0)
-        nc.scalar.dma_start(xs_table[0:P:8, :].bitcast(I32), x_scales[0].bitcast(I32))
+        nc.vector.memset(xs_table[:, 0:ZERO_SPLIT].bitcast(I32), 0)
+        nc.gpsimd.memset(xs_table[:, ZERO_SPLIT:T].bitcast(I32), 0)
 
         w1_rows = w1.rearrange("(p j) c -> p j c", j=PACK)
-        w1_raw = []
-        for u in range(2):
-            raw = keep.tile([P, PACK, H // 2], F32, name=f"w1_raw{u}")
-            nc.sync.dma_start(raw[:], w1_rows[:, :, u * (H // 2) : (u + 1) * (H // 2)])
-            w1_raw.append(raw)
-
+        w1_raw = [keep.tile([P, PACK, hi - lo], F32, name=f"w1_raw{lo}") for lo, hi in W1_PIECES]
+        nc.sync.dma_start(w1_raw[0][:], w1_rows[:, :, W1_PIECES[0][0] : W1_PIECES[0][1]])
+        offsets = keep.tile([P, S // 16], U16, name="offsets")
+        nc.sync.dma_start(offsets[:], offs)
+        nc.sync.dma_start(w1_raw[1][:], w1_rows[:, :, W1_PIECES[1][0] : W1_PIECES[1][1]])
+        w2_codes = keep.tile([P, 2 * N], U8, name="w2_codes", align_bytes=64)
+        nc.sync.dma_start(w2_codes[:].bitcast(I32), w2_words[0].bitcast(I32))
+        nc.sync.dma_start(xs_table[0:P:8, :].bitcast(I32), x_scales[0].bitcast(I32))
+        nc.sync.dma_start(w1_raw[2][:], w1_rows[:, :, W1_PIECES[2][0] : W1_PIECES[2][1]])
         xw_table = keep.tile([P, T], U32, name="xw_table", align_bytes=64)
         nc.sync.dma_start(xw_table[:].bitcast(I32), x_words[0].rearrange("p n t -> p (n t)").bitcast(I32))
 
-        w2_codes = keep.tile([P, 2 * N], U8, name="w2_codes", align_bytes=64)
-        nc.sync.dma_start(w2_codes[:].bitcast(I32), w2_words[0].bitcast(I32))
         w2_plane = keep.tile([P, N], U8, name="w2_plane", align_bytes=64)
         nc.gpsimd.memset(w2_plane[:].bitcast(I32), 0)
         for q in range(4):
             nc.gpsimd.dma_start(w2_plane[32 * q : 32 * q + 4, :].bitcast(I32), w2_scales[0, 4 * q : 4 * q + 4, :].bitcast(I32))
 
-        xs_plane = keep.tile([P, S], U8, name="xs_plane", align_bytes=64)
-        nc.vector.memset(xs_plane[:].bitcast(I32), 0)
-        xs_picked = keep.tile([P, S], U8, name="xs_picked", align_bytes=64)
-        nc.vector.tensor_copy(xs_picked[:], xs_table[:].indirect(offsets[:]))
-        for r in range(4):
-            nc.sync.dma_start(xs_plane[r:P:32, :].bitcast(I32), xs_picked[8 * r : P : 32, :].bitcast(I32))
+        xs_plane = []
+        for v in range(S // HALF):
+            plane = keep.tile([P, HALF], U8, name=f"xs_plane{v}", align_bytes=64)
+            nc.vector.memset(plane[:].bitcast(I32), 0)
+            picked = keep.tile([P, HALF], U8, name=f"xs_picked{v}", align_bytes=64)
+            nc.vector.tensor_copy(picked[:], xs_table[:].indirect(offsets[:, v * (HALF // 16) : (v + 1) * (HALF // 16)]))
+            for r in range(4):
+                nc.sync.dma_start(plane[r:P:32, :].bitcast(I32), picked[8 * r : P : 32, :].bitcast(I32))
+            xs_plane.append(plane)
 
         w1_bf = keep.tile([P, PACK, P, PACK], BF16, name="w1_bf", align_bytes=64)
-        for u in range(2):
-            dst = w1_bf[:, :, 64 * u : 64 * (u + 1), :].rearrange("p t m j -> p m t j")
-            src = w1_raw[u][:].rearrange("p j (m t) -> p m t j", t=PACK)
-            if u == 0:
-                nc.scalar.copy(dst, src)
-            else:
-                nc.scalar.copy(dst[:, 0:24], src[:, 0:24])
-                nc.vector.tensor_copy(dst[:, 24:64], src[:, 24:64])
+        for raw, (lo, hi) in zip(w1_raw, W1_PIECES):
+            dst = w1_bf[:, :, lo // PACK : hi // PACK, :].rearrange("p t m j -> p m t j")
+            src = raw[:].rearrange("p j (m t) -> p m t j", t=PACK)
+            nc.scalar.copy(dst, src)
         w1_codes = keep.tile([P, H], U32, name="w1_codes", align_bytes=64)
         w1_plane = keep.tile([P, H], U8, name="w1_plane", align_bytes=64)
         nc.vector.quantize_mx(out=w1_codes[:].bitcast(FP8X4), scales=w1_plane[:], in_=w1_bf[:].rearrange("p t m j -> p (t m j)"))
+
+        warm = psum.tile([P, H], F32, name="warm", tag="bank")
+        for w in range(WARM):
+            nc.tensor.matmul_mx(
+                out=warm[:],
+                lhsT=w1_codes[:, w * P : (w + 1) * P].bitcast(FP8X4),
+                lhsT_scale=w1_plane[:, w * P : (w + 1) * P],
+                rhs=w1_codes[:].bitcast(FP8X4),
+                rhs_scale=w1_plane[:],
+                start=True,
+                stop=True,
+            )
 
         xw_picked = []
         for u in range(S // UNIT):
@@ -84,6 +97,7 @@ def tile_picked_phmlp_relu_p_kernel(tc, x_words, x_scales, w1, w2_words, w2_scal
 
         def first_layer(c):
             u, e = divmod(c, UNIT // CHUNK)
+            v, f = divmod(c, HALF // CHUNK)
             bank = psum.tile([P, PACK, CHUNK], F32, name="h_bank", tag="bank")
             for t in range(PACK):
                 nc.tensor.matmul_mx(
@@ -91,7 +105,7 @@ def tile_picked_phmlp_relu_p_kernel(tc, x_words, x_scales, w1, w2_words, w2_scal
                     lhsT=w1_codes[:, t * P : (t + 1) * P].bitcast(FP8X4),
                     lhsT_scale=w1_plane[:, t * P : (t + 1) * P],
                     rhs=xw_picked[u][:, e * CHUNK : (e + 1) * CHUNK].bitcast(FP8X4),
-                    rhs_scale=xs_plane[:, c * CHUNK : (c + 1) * CHUNK],
+                    rhs_scale=xs_plane[v][:, f * CHUNK : (f + 1) * CHUNK],
                     start=True,
                     stop=True,
                 )
@@ -121,15 +135,14 @@ def tile_picked_phmlp_relu_p_kernel(tc, x_words, x_scales, w1, w2_words, w2_scal
 
         for c in range(S // CHUNK):
             first_layer(c)
-        last = S // UNIT - 1
         for u in range(S // UNIT):
             h_codes, h_plane = quantise_hidden(u)
             res = keep.tile([P, N // P, UNIT], F32, name=f"res{u}")
-            if u < last:
+            if u < 2:
                 bank = psum.tile([P, N // P, UNIT], F32, name="o_bank", tag="bank")
                 for a in range(N // P):
                     second_pass(bank[:, a, :], a, h_codes, h_plane)
-                if u == 1:
+                if u == 0:
                     nc.vector.tensor_copy(res[:], bank[:])
                 else:
                     nc.scalar.copy(res[:], bank[:])

@@ -22,8 +22,8 @@ HALF = 512
 CHUNK = 128
 VECTOR_RELU = (2, 4)
 ZERO_SPLIT = 1280
-WARM = 1
-W1_PIECES = ((0, 128), (128, 256), (256, 512))
+WARM = 2
+W1_PIECES = ((0, 128), (128, 256), (256, 384), (384, 512))
 
 
 def tile_picked_phmlp_relu_p_kernel(tc, x_words, x_scales, w1, w2_words, w2_scales, offs, out):
@@ -46,29 +46,33 @@ def tile_picked_phmlp_relu_p_kernel(tc, x_words, x_scales, w1, w2_words, w2_scal
         nc.sync.dma_start(w2_codes[:].bitcast(I32), w2_words[0].bitcast(I32))
         nc.sync.dma_start(xs_table[0:P:8, :].bitcast(I32), x_scales[0].bitcast(I32))
         nc.sync.dma_start(w1_raw[2][:], w1_rows[:, :, W1_PIECES[2][0] : W1_PIECES[2][1]])
+        nc.sync.dma_start(w1_raw[3][:], w1_rows[:, :, W1_PIECES[3][0] : W1_PIECES[3][1]])
         xw_table = keep.tile([P, T], U32, name="xw_table", align_bytes=64)
         nc.sync.dma_start(xw_table[:].bitcast(I32), x_words[0].rearrange("p n t -> p (n t)").bitcast(I32))
-
-        w2_plane = keep.tile([P, N], U8, name="w2_plane", align_bytes=64)
-        nc.gpsimd.memset(w2_plane[:].bitcast(I32), 0)
-        for q in range(4):
-            nc.gpsimd.dma_start(w2_plane[32 * q : 32 * q + 4, :].bitcast(I32), w2_scales[0, 4 * q : 4 * q + 4, :].bitcast(I32))
 
         xs_plane = []
         for v in range(S // HALF):
             plane = keep.tile([P, HALF], U8, name=f"xs_plane{v}", align_bytes=64)
             nc.vector.memset(plane[:].bitcast(I32), 0)
-            picked = keep.tile([P, HALF], U8, name=f"xs_picked{v}", align_bytes=64)
+            picked = keep.tile([P, HALF], U8, name=f"xs_picked{v}", tag="in_turn", bufs=3, align_bytes=64)
             nc.vector.tensor_copy(picked[:], xs_table[:].indirect(offsets[:, v * (HALF // 16) : (v + 1) * (HALF // 16)]))
             for r in range(4):
                 nc.sync.dma_start(plane[r:P:32, :].bitcast(I32), picked[8 * r : P : 32, :].bitcast(I32))
             xs_plane.append(plane)
 
+        w2_plane = keep.tile([P, N], U8, name="w2_plane", tag="in_turn", bufs=3, align_bytes=64)
+        nc.gpsimd.memset(w2_plane[:].bitcast(I32), 0)
+        for q in range(4):
+            nc.sync.dma_start(w2_plane[32 * q : 32 * q + 4, :].bitcast(I32), w2_scales[0, 4 * q : 4 * q + 4, :].bitcast(I32))
+
         w1_bf = keep.tile([P, PACK, P, PACK], BF16, name="w1_bf", align_bytes=64)
         for raw, (lo, hi) in zip(w1_raw, W1_PIECES):
             dst = w1_bf[:, :, lo // PACK : hi // PACK, :].rearrange("p t m j -> p m t j")
             src = raw[:].rearrange("p j (m t) -> p m t j", t=PACK)
-            nc.scalar.copy(dst, src)
+            if lo == 0:
+                nc.vector.tensor_copy(dst, src)
+            else:
+                nc.scalar.copy(dst, src)
         w1_codes = keep.tile([P, H], U32, name="w1_codes", align_bytes=64)
         w1_plane = keep.tile([P, H], U8, name="w1_plane", align_bytes=64)
         nc.vector.quantize_mx(out=w1_codes[:].bitcast(FP8X4), scales=w1_plane[:], in_=w1_bf[:].rearrange("p t m j -> p (t m j)"))
@@ -117,7 +121,7 @@ def tile_picked_phmlp_relu_p_kernel(tc, x_words, x_scales, w1, w2_words, w2_scal
                 nc.scalar.activation(dst, src, RELU)
 
         def quantise_hidden(u):
-            h_codes = keep.tile([P, UNIT], U32, name=f"h_codes{u}", align_bytes=64)
+            h_codes = keep.tile([P, UNIT], U32, name=f"h_codes{u}", tag="vector_turn", bufs=5, align_bytes=64)
             h_plane = keep.tile([P, UNIT], U8, name=f"h_plane{u}", align_bytes=64)
             nc.vector.quantize_mx(out=h_codes[:].bitcast(FP8X4), scales=h_plane[:], in_=h_bf[u][:].rearrange("p n t -> p (n t)"))
             return h_codes, h_plane
@@ -135,9 +139,15 @@ def tile_picked_phmlp_relu_p_kernel(tc, x_words, x_scales, w1, w2_words, w2_scal
 
         for c in range(S // CHUNK):
             first_layer(c)
+        hidden = [quantise_hidden(0)]
         for u in range(S // UNIT):
-            h_codes, h_plane = quantise_hidden(u)
-            res = keep.tile([P, N // P, UNIT], F32, name=f"res{u}")
+            if u + 1 < S // UNIT:
+                hidden.append(quantise_hidden(u + 1))
+            h_codes, h_plane = hidden[u]
+            if u == 0:
+                res = keep.tile([P, N // P, UNIT], F32, name="res0", tag="vector_turn", bufs=5, align_bytes=64)
+            else:
+                res = keep.tile([P, N // P, UNIT], F32, name=f"res{u}")
             if u < 2:
                 bank = psum.tile([P, N // P, UNIT], F32, name="o_bank", tag="bank")
                 for a in range(N // P):

@@ -21,9 +21,8 @@ UNIT = 256
 HALF = 512
 CHUNK = 128
 VECTOR_RELU = (2, 4)
-ZERO_SPLIT = 1280
-WARM = 2
-W1_PIECES = ((0, 128), (128, 256), (256, 384), (384, 512))
+WARM = 1
+CAST_SPLIT = 64
 
 
 def tile_picked_phmlp_relu_p_kernel(tc, x_words, x_scales, w1, w2_words, w2_scales, offs, out):
@@ -33,32 +32,28 @@ def tile_picked_phmlp_relu_p_kernel(tc, x_words, x_scales, w1, w2_words, w2_scal
         psum = ctx.enter_context(tc.psum_pool(name="psum", bufs=8))
 
         xs_table = keep.tile([P, T], U8, name="xs_table", align_bytes=64)
-        nc.vector.memset(xs_table[:, 0:ZERO_SPLIT].bitcast(I32), 0)
-        nc.gpsimd.memset(xs_table[:, ZERO_SPLIT:T].bitcast(I32), 0)
+        nc.vector.memset(xs_table[:].bitcast(I32), 0)
+        xs_plane = []
+        for v in range(S // HALF):
+            plane = keep.tile([P, HALF], U8, name=f"xs_plane{v}", tag="load_turn", bufs=4, align_bytes=64)
+            nc.vector.memset(plane[:].bitcast(I32), 0)
+            xs_plane.append(plane)
 
-        w1_rows = w1.rearrange("(p j) c -> p j c", j=PACK)
-        w1_raw = [keep.tile([P, PACK, hi - lo], F32, name=f"w1_raw{lo}") for lo, hi in W1_PIECES]
-        nc.sync.dma_start(w1_raw[0][:], w1_rows[:, :, W1_PIECES[0][0] : W1_PIECES[0][1]])
         offsets = keep.tile([P, S // 16], U16, name="offsets")
         nc.sync.dma_start(offsets[:], offs)
-        nc.sync.dma_start(w1_raw[1][:], w1_rows[:, :, W1_PIECES[1][0] : W1_PIECES[1][1]])
         w2_codes = keep.tile([P, 2 * N], U8, name="w2_codes", align_bytes=64)
         nc.sync.dma_start(w2_codes[:].bitcast(I32), w2_words[0].bitcast(I32))
         nc.sync.dma_start(xs_table[0:P:8, :].bitcast(I32), x_scales[0].bitcast(I32))
-        nc.sync.dma_start(w1_raw[2][:], w1_rows[:, :, W1_PIECES[2][0] : W1_PIECES[2][1]])
-        nc.sync.dma_start(w1_raw[3][:], w1_rows[:, :, W1_PIECES[3][0] : W1_PIECES[3][1]])
-        xw_table = keep.tile([P, T], U32, name="xw_table", align_bytes=64)
+        w1_raw = keep.tile([P, PACK, H], F32, name="w1_raw", tag="load_turn", bufs=4, align_bytes=64)
+        nc.sync.dma_start(w1_raw[:], w1.rearrange("(p j) c -> p j c", j=PACK))
+        xw_table = keep.tile([P, T], U32, name="xw_table", tag="load_turn", bufs=4, align_bytes=64)
         nc.sync.dma_start(xw_table[:].bitcast(I32), x_words[0].rearrange("p n t -> p (n t)").bitcast(I32))
 
-        xs_plane = []
         for v in range(S // HALF):
-            plane = keep.tile([P, HALF], U8, name=f"xs_plane{v}", align_bytes=64)
-            nc.vector.memset(plane[:].bitcast(I32), 0)
             picked = keep.tile([P, HALF], U8, name=f"xs_picked{v}", tag="in_turn", bufs=3, align_bytes=64)
             nc.vector.tensor_copy(picked[:], xs_table[:].indirect(offsets[:, v * (HALF // 16) : (v + 1) * (HALF // 16)]))
             for r in range(4):
-                nc.sync.dma_start(plane[r:P:32, :].bitcast(I32), picked[8 * r : P : 32, :].bitcast(I32))
-            xs_plane.append(plane)
+                nc.sync.dma_start(xs_plane[v][r:P:32, :].bitcast(I32), picked[8 * r : P : 32, :].bitcast(I32))
 
         w2_plane = keep.tile([P, N], U8, name="w2_plane", tag="in_turn", bufs=3, align_bytes=64)
         nc.gpsimd.memset(w2_plane[:].bitcast(I32), 0)
@@ -66,14 +61,11 @@ def tile_picked_phmlp_relu_p_kernel(tc, x_words, x_scales, w1, w2_words, w2_scal
             nc.sync.dma_start(w2_plane[32 * q : 32 * q + 4, :].bitcast(I32), w2_scales[0, 4 * q : 4 * q + 4, :].bitcast(I32))
 
         w1_bf = keep.tile([P, PACK, P, PACK], BF16, name="w1_bf", align_bytes=64)
-        for raw, (lo, hi) in zip(w1_raw, W1_PIECES):
-            dst = w1_bf[:, :, lo // PACK : hi // PACK, :].rearrange("p t m j -> p m t j")
-            src = raw[:].rearrange("p j (m t) -> p m t j", t=PACK)
-            if lo == 0:
-                nc.vector.tensor_copy(dst, src)
-            else:
-                nc.scalar.copy(dst, src)
-        w1_codes = keep.tile([P, H], U32, name="w1_codes", align_bytes=64)
+        w1_dst = w1_bf[:].rearrange("p t m j -> p m t j")
+        w1_src = w1_raw[:].rearrange("p j (m t) -> p m t j", t=PACK)
+        nc.scalar.copy(w1_dst[:, 0:CAST_SPLIT], w1_src[:, 0:CAST_SPLIT])
+        nc.vector.tensor_copy(w1_dst[:, CAST_SPLIT:P], w1_src[:, CAST_SPLIT:P])
+        w1_codes = keep.tile([P, H], U32, name="w1_codes", tag="vector_turn", bufs=10, align_bytes=64)
         w1_plane = keep.tile([P, H], U8, name="w1_plane", align_bytes=64)
         nc.vector.quantize_mx(out=w1_codes[:].bitcast(FP8X4), scales=w1_plane[:], in_=w1_bf[:].rearrange("p t m j -> p (t m j)"))
 
@@ -91,7 +83,7 @@ def tile_picked_phmlp_relu_p_kernel(tc, x_words, x_scales, w1, w2_words, w2_scal
 
         xw_picked = []
         for u in range(S // UNIT):
-            g = keep.tile([P, UNIT], U32, name=f"xw_picked{u}", align_bytes=64)
+            g = keep.tile([P, UNIT], U32, name=f"xw_picked{u}", tag="vector_turn", bufs=10, align_bytes=64)
             nc.vector.tensor_copy(g[:], xw_table[:].indirect(offsets[:, u * (UNIT // 16) : (u + 1) * (UNIT // 16)]))
             xw_picked.append(g)
 
@@ -121,7 +113,7 @@ def tile_picked_phmlp_relu_p_kernel(tc, x_words, x_scales, w1, w2_words, w2_scal
                 nc.scalar.activation(dst, src, RELU)
 
         def quantise_hidden(u):
-            h_codes = keep.tile([P, UNIT], U32, name=f"h_codes{u}", tag="vector_turn", bufs=5, align_bytes=64)
+            h_codes = keep.tile([P, UNIT], U32, name=f"h_codes{u}", tag="vector_turn", bufs=10, align_bytes=64)
             h_plane = keep.tile([P, UNIT], U8, name=f"h_plane{u}", align_bytes=64)
             nc.vector.quantize_mx(out=h_codes[:].bitcast(FP8X4), scales=h_plane[:], in_=h_bf[u][:].rearrange("p n t -> p (n t)"))
             return h_codes, h_plane
@@ -145,7 +137,7 @@ def tile_picked_phmlp_relu_p_kernel(tc, x_words, x_scales, w1, w2_words, w2_scal
                 hidden.append(quantise_hidden(u + 1))
             h_codes, h_plane = hidden[u]
             if u == 0:
-                res = keep.tile([P, N // P, UNIT], F32, name="res0", tag="vector_turn", bufs=5, align_bytes=64)
+                res = keep.tile([P, N // P, UNIT], F32, name="res0", tag="vector_turn", bufs=10, align_bytes=64)
             else:
                 res = keep.tile([P, N // P, UNIT], F32, name=f"res{u}")
             if u < 2:

@@ -17,103 +17,108 @@ RELU = mybir.ActivationFunctionType.Relu
 
 P = 128
 PACK = 4
-UNIT = 256
+QUAD = 32
+GROUP = 16
+BLOCK_ROWS = 8
+BANKS = 8
+
 HALF = 512
+UNIT = 256
 CHUNK = 128
+HALVES, UNITS, CHUNKS = S // HALF, S // UNIT, S // CHUNK
+OUT_BLOCKS = N // P
+
 VECTOR_RELU = (2, 4)
-WARM = 1
-CAST_SPLIT = 64
+CAST_SPLIT = 80
+FIRST_SHARED_UNIT = 2
 
 
 def tile_picked_phmlp_relu_p_kernel(tc, x_words, x_scales, w1, w2_words, w2_scales, offs, out):
     nc = tc.nc
     with ExitStack() as ctx:
         keep = ctx.enter_context(tc.tile_pool(name="keep", bufs=1))
-        psum = ctx.enter_context(tc.psum_pool(name="psum", bufs=8))
+        psum = ctx.enter_context(tc.psum_pool(name="psum", bufs=BANKS))
+
+        load_turn = dict(tag="load_turn", bufs=HALVES + 3, align_bytes=64)
+        byte_turn = dict(tag="byte_turn", bufs=HALVES + 1, align_bytes=64)
+        vector_turn = dict(tag="vector_turn", bufs=2 * UNITS + 2, align_bytes=64)
 
         xs_table = keep.tile([P, T], U8, name="xs_table", align_bytes=64)
         nc.vector.memset(xs_table[:].bitcast(I32), 0)
-        xs_plane = []
-        for v in range(S // HALF):
-            plane = keep.tile([P, HALF], U8, name=f"xs_plane{v}", tag="load_turn", bufs=4, align_bytes=64)
-            nc.vector.memset(plane[:].bitcast(I32), 0)
-            xs_plane.append(plane)
+        xs_planes = []
+        for v in range(HALVES):
+            xs_plane = keep.tile([P, HALF], U8, name=f"xs_plane{v}", **load_turn)
+            nc.vector.memset(xs_plane[:].bitcast(I32), 0)
+            xs_planes.append(xs_plane)
 
-        offsets = keep.tile([P, S // 16], U16, name="offsets")
+        w1_rows = w1.rearrange("(p j) c -> p j c", j=PACK)
+        w1_head = keep.tile([P, 1, H], F32, name="w1_head")
+        nc.sync.dma_start(w1_head[:], w1_rows[:, 0:1, :])
+        offsets = keep.tile([P, S // GROUP], U16, name="offsets")
         nc.sync.dma_start(offsets[:], offs)
-        w2_codes = keep.tile([P, 2 * N], U8, name="w2_codes", align_bytes=64)
-        nc.sync.dma_start(w2_codes[:].bitcast(I32), w2_words[0].bitcast(I32))
-        nc.sync.dma_start(xs_table[0:P:8, :].bitcast(I32), x_scales[0].bitcast(I32))
-        w1_raw = keep.tile([P, PACK, H], F32, name="w1_raw", tag="load_turn", bufs=4, align_bytes=64)
-        nc.sync.dma_start(w1_raw[:], w1.rearrange("(p j) c -> p j c", j=PACK))
-        xw_table = keep.tile([P, T], U32, name="xw_table", tag="load_turn", bufs=4, align_bytes=64)
+        nc.sync.dma_start(xs_table[0:P:BLOCK_ROWS, :].bitcast(I32), x_scales[0].bitcast(I32))
+        w1_rest = keep.tile([P, PACK - 1, H], F32, name="w1_rest", **load_turn)
+        nc.sync.dma_start(w1_rest[:], w1_rows[:, 1:PACK, :])
+        xw_table = keep.tile([P, T], U32, name="xw_table", **load_turn)
         nc.sync.dma_start(xw_table[:].bitcast(I32), x_words[0].rearrange("p n t -> p (n t)").bitcast(I32))
+        w2_codes = keep.tile([P, 2 * N], U8, name="w2_codes", **load_turn)
+        nc.sync.dma_start(w2_codes[:].bitcast(I32), w2_words[0].bitcast(I32))
 
-        for v in range(S // HALF):
-            picked = keep.tile([P, HALF], U8, name=f"xs_picked{v}", tag="in_turn", bufs=3, align_bytes=64)
-            nc.vector.tensor_copy(picked[:], xs_table[:].indirect(offsets[:, v * (HALF // 16) : (v + 1) * (HALF // 16)]))
-            for r in range(4):
-                nc.sync.dma_start(xs_plane[v][r:P:32, :].bitcast(I32), picked[8 * r : P : 32, :].bitcast(I32))
+        for v in range(HALVES):
+            xs_picked = keep.tile([P, HALF], U8, name=f"xs_picked{v}", **byte_turn)
+            entries = offsets[:, v * (HALF // GROUP) : (v + 1) * (HALF // GROUP)]
+            nc.vector.tensor_copy(xs_picked[:], xs_table[:].indirect(entries))
+            for r in range(QUAD // BLOCK_ROWS):
+                nc.sync.dma_start(xs_planes[v][r:P:QUAD, :].bitcast(I32), xs_picked[BLOCK_ROWS * r : P : QUAD, :].bitcast(I32))
 
-        w2_plane = keep.tile([P, N], U8, name="w2_plane", tag="in_turn", bufs=3, align_bytes=64)
+        w2_plane = keep.tile([P, N], U8, name="w2_plane", **byte_turn)
         nc.gpsimd.memset(w2_plane[:].bitcast(I32), 0)
-        for q in range(4):
-            nc.sync.dma_start(w2_plane[32 * q : 32 * q + 4, :].bitcast(I32), w2_scales[0, 4 * q : 4 * q + 4, :].bitcast(I32))
+        for q in range(P // QUAD):
+            nc.sync.dma_start(w2_plane[QUAD * q : QUAD * q + 4, :].bitcast(I32), w2_scales[0, 4 * q : 4 * q + 4, :].bitcast(I32))
 
         w1_bf = keep.tile([P, PACK, P, PACK], BF16, name="w1_bf", align_bytes=64)
         w1_dst = w1_bf[:].rearrange("p t m j -> p m t j")
-        w1_src = w1_raw[:].rearrange("p j (m t) -> p m t j", t=PACK)
-        nc.scalar.copy(w1_dst[:, 0:CAST_SPLIT], w1_src[:, 0:CAST_SPLIT])
-        nc.vector.tensor_copy(w1_dst[:, CAST_SPLIT:P], w1_src[:, CAST_SPLIT:P])
-        w1_codes = keep.tile([P, H], U32, name="w1_codes", tag="vector_turn", bufs=10, align_bytes=64)
+        for w1_part, rows in ((w1_head, slice(0, 1)), (w1_rest, slice(1, PACK))):
+            w1_src = w1_part[:].rearrange("p j (m t) -> p m t j", t=PACK)
+            nc.scalar.copy(w1_dst[:, 0:CAST_SPLIT, :, rows], w1_src[:, 0:CAST_SPLIT])
+            nc.vector.tensor_copy(w1_dst[:, CAST_SPLIT:P, :, rows], w1_src[:, CAST_SPLIT:P])
+        w1_codes = keep.tile([P, H], U32, name="w1_codes", **vector_turn)
         w1_plane = keep.tile([P, H], U8, name="w1_plane", align_bytes=64)
         nc.vector.quantize_mx(out=w1_codes[:].bitcast(FP8X4), scales=w1_plane[:], in_=w1_bf[:].rearrange("p t m j -> p (t m j)"))
 
-        warm = psum.tile([P, H], F32, name="warm", tag="bank")
-        for w in range(WARM):
-            nc.tensor.matmul_mx(
-                out=warm[:],
-                lhsT=w1_codes[:, w * P : (w + 1) * P].bitcast(FP8X4),
-                lhsT_scale=w1_plane[:, w * P : (w + 1) * P],
-                rhs=w1_codes[:].bitcast(FP8X4),
-                rhs_scale=w1_plane[:],
-                start=True,
-                stop=True,
-            )
-
         xw_picked = []
-        for u in range(S // UNIT):
-            g = keep.tile([P, UNIT], U32, name=f"xw_picked{u}", tag="vector_turn", bufs=10, align_bytes=64)
-            nc.vector.tensor_copy(g[:], xw_table[:].indirect(offsets[:, u * (UNIT // 16) : (u + 1) * (UNIT // 16)]))
-            xw_picked.append(g)
+        for u in range(UNITS):
+            words = keep.tile([P, UNIT], U32, name=f"xw_picked{u}", **vector_turn)
+            entries = offsets[:, u * (UNIT // GROUP) : (u + 1) * (UNIT // GROUP)]
+            nc.vector.tensor_copy(words[:], xw_table[:].indirect(entries))
+            xw_picked.append(words)
 
         out_rows = out.rearrange("(a p) s -> p a s", p=P)
-
-        h_bf = [keep.tile([P, UNIT, PACK], BF16, name=f"h_bf{u}", align_bytes=64) for u in range(S // UNIT)]
+        h_bf = [keep.tile([P, UNIT, PACK], BF16, name=f"h_bf{u}", align_bytes=64) for u in range(UNITS)]
 
         def first_layer(c):
-            u, e = divmod(c, UNIT // CHUNK)
-            v, f = divmod(c, HALF // CHUNK)
-            bank = psum.tile([P, PACK, CHUNK], F32, name="h_bank", tag="bank")
+            u, in_unit = divmod(c, UNIT // CHUNK)
+            v, in_half = divmod(c, HALF // CHUNK)
+            h_bank = psum.tile([P, PACK, CHUNK], F32, name="h_bank", tag="bank")
             for t in range(PACK):
                 nc.tensor.matmul_mx(
-                    out=bank[:, t, :],
+                    out=h_bank[:, t, :],
                     lhsT=w1_codes[:, t * P : (t + 1) * P].bitcast(FP8X4),
                     lhsT_scale=w1_plane[:, t * P : (t + 1) * P],
-                    rhs=xw_picked[u][:, e * CHUNK : (e + 1) * CHUNK].bitcast(FP8X4),
-                    rhs_scale=xs_plane[v][:, f * CHUNK : (f + 1) * CHUNK],
+                    rhs=xw_picked[u][:, in_unit * CHUNK : (in_unit + 1) * CHUNK].bitcast(FP8X4),
+                    rhs_scale=xs_planes[v][:, in_half * CHUNK : (in_half + 1) * CHUNK],
                     start=True,
                     stop=True,
                 )
-            dst = h_bf[u][:, e * CHUNK : (e + 1) * CHUNK, :]
-            src = bank[:].rearrange("p t n -> p n t")
+            h_dst = h_bf[u][:, in_unit * CHUNK : (in_unit + 1) * CHUNK, :]
+            h_src = h_bank[:].rearrange("p t n -> p n t")
             if c in VECTOR_RELU:
-                nc.vector.tensor_scalar_max(dst, src, 0.0)
+                nc.vector.tensor_scalar_max(h_dst, h_src, 0.0)
             else:
-                nc.scalar.activation(dst, src, RELU)
+                nc.scalar.activation(h_dst, h_src, RELU)
 
         def quantise_hidden(u):
-            h_codes = keep.tile([P, UNIT], U32, name=f"h_codes{u}", tag="vector_turn", bufs=10, align_bytes=64)
+            h_codes = keep.tile([P, UNIT], U32, name=f"h_codes{u}", **vector_turn)
             h_plane = keep.tile([P, UNIT], U8, name=f"h_plane{u}", align_bytes=64)
             nc.vector.quantize_mx(out=h_codes[:].bitcast(FP8X4), scales=h_plane[:], in_=h_bf[u][:].rearrange("p n t -> p (n t)"))
             return h_codes, h_plane
@@ -129,31 +134,33 @@ def tile_picked_phmlp_relu_p_kernel(tc, x_words, x_scales, w1, w2_words, w2_scal
                 stop=True,
             )
 
-        for c in range(S // CHUNK):
+        for c in range(CHUNKS - 1):
             first_layer(c)
         hidden = [quantise_hidden(0)]
-        for u in range(S // UNIT):
-            if u + 1 < S // UNIT:
+        for u in range(UNITS):
+            if u + 1 < UNITS:
                 hidden.append(quantise_hidden(u + 1))
             h_codes, h_plane = hidden[u]
             if u == 0:
-                res = keep.tile([P, N // P, UNIT], F32, name="res0", tag="vector_turn", bufs=10, align_bytes=64)
+                result = keep.tile([P, OUT_BLOCKS, UNIT], F32, name="result0", **vector_turn)
             else:
-                res = keep.tile([P, N // P, UNIT], F32, name=f"res{u}")
-            if u < 2:
-                bank = psum.tile([P, N // P, UNIT], F32, name="o_bank", tag="bank")
-                for a in range(N // P):
-                    second_pass(bank[:, a, :], a, h_codes, h_plane)
+                result = keep.tile([P, OUT_BLOCKS, UNIT], F32, name=f"result{u}")
+            if u < FIRST_SHARED_UNIT:
+                out_bank = psum.tile([P, OUT_BLOCKS, UNIT], F32, name="out_bank", tag="bank")
+                for a in range(OUT_BLOCKS):
+                    second_pass(out_bank[:, a, :], a, h_codes, h_plane)
                 if u == 0:
-                    nc.vector.tensor_copy(res[:], bank[:])
+                    nc.vector.tensor_copy(result[:], out_bank[:])
                 else:
-                    nc.scalar.copy(res[:], bank[:])
+                    nc.scalar.copy(result[:], out_bank[:])
             else:
-                for a in range(N // P):
-                    bank = psum.tile([P, UNIT], F32, name="o_half", tag="bank")
-                    second_pass(bank[:], a, h_codes, h_plane)
+                for a in range(OUT_BLOCKS):
+                    block_bank = psum.tile([P, UNIT], F32, name="block_bank", tag="bank")
+                    second_pass(block_bank[:], a, h_codes, h_plane)
                     if a == 0:
-                        nc.vector.tensor_copy(res[:, a, :], bank[:])
+                        nc.vector.tensor_copy(result[:, a, :], block_bank[:])
                     else:
-                        nc.scalar.copy(res[:, a, :], bank[:])
-            nc.sync.dma_start(out_rows[:, :, u * UNIT : (u + 1) * UNIT], res[:])
+                        nc.scalar.copy(result[:, a, :], block_bank[:])
+            nc.sync.dma_start(out_rows[:, :, u * UNIT : (u + 1) * UNIT], result[:])
+            if u == 0:
+                first_layer(CHUNKS - 1)

@@ -22,15 +22,13 @@ GROUP = 16
 BLOCK_ROWS = 8
 BANKS = 8
 
-HALF = 512
 UNIT = 256
 CHUNK = 128
-HALVES, UNITS, CHUNKS = S // HALF, S // UNIT, S // CHUNK
+UNITS, CHUNKS = S // UNIT, S // CHUNK
 OUT_BLOCKS = N // P
-
-VECTOR_RELU = (2, 4)
-CAST_SPLIT = 80
-FIRST_SHARED_UNIT = 2
+EARLY = 512
+CAST_SPLIT = 64
+WARM = (512, 256)
 
 
 def tile_picked_phmlp_relu_p_kernel(tc, x_words, x_scales, w1, w2_words, w2_scales, offs, out):
@@ -39,66 +37,71 @@ def tile_picked_phmlp_relu_p_kernel(tc, x_words, x_scales, w1, w2_words, w2_scal
         keep = ctx.enter_context(tc.tile_pool(name="keep", bufs=1))
         psum = ctx.enter_context(tc.psum_pool(name="psum", bufs=BANKS))
 
-        load_turn = dict(tag="load_turn", bufs=HALVES + 3, align_bytes=64)
-        byte_turn = dict(tag="byte_turn", bufs=HALVES + 1, align_bytes=64)
-        vector_turn = dict(tag="vector_turn", bufs=2 * UNITS + 2, align_bytes=64)
+        load_turn = dict(tag="load_turn", bufs=5, align_bytes=64)
+        vector_turn = dict(tag="vector_turn", bufs=20, align_bytes=64)
 
         xs_table = keep.tile([P, T], U8, name="xs_table", align_bytes=64)
         nc.vector.memset(xs_table[:].bitcast(I32), 0)
+        parts = ((0, EARLY), (EARLY, S))
         xs_planes = []
-        for v in range(HALVES):
-            xs_plane = keep.tile([P, HALF], U8, name=f"xs_plane{v}", **load_turn)
+        for v, (lo, hi) in enumerate(parts):
+            xs_plane = keep.tile([P, hi - lo], U8, name=f"xs_plane{v}", **load_turn)
             nc.vector.memset(xs_plane[:].bitcast(I32), 0)
             xs_planes.append(xs_plane)
 
         w1_rows = w1.rearrange("(p j) c -> p j c", j=PACK)
-        w1_head = keep.tile([P, 1, H], F32, name="w1_head")
-        nc.sync.dma_start(w1_head[:], w1_rows[:, 0:1, :])
+        w1_head = keep.tile([P, PACK, H // 2], F32, name="w1_head")
+        nc.sync.dma_start(w1_head[:], w1_rows[:, :, 0 : H // 2])
         offsets = keep.tile([P, S // GROUP], U16, name="offsets")
         nc.sync.dma_start(offsets[:], offs)
         nc.sync.dma_start(xs_table[0:P:BLOCK_ROWS, :].bitcast(I32), x_scales[0].bitcast(I32))
-        w1_rest = keep.tile([P, PACK - 1, H], F32, name="w1_rest", **load_turn)
-        nc.sync.dma_start(w1_rest[:], w1_rows[:, 1:PACK, :])
+        w1_rest = keep.tile([P, PACK, H // 2], F32, name="w1_rest", **load_turn)
+        nc.sync.dma_start(w1_rest[:], w1_rows[:, :, H // 2 : H])
         xw_table = keep.tile([P, T], U32, name="xw_table", **load_turn)
         nc.sync.dma_start(xw_table[:].bitcast(I32), x_words[0].rearrange("p n t -> p (n t)").bitcast(I32))
         w2_codes = keep.tile([P, 2 * N], U8, name="w2_codes", **load_turn)
         nc.sync.dma_start(w2_codes[:].bitcast(I32), w2_words[0].bitcast(I32))
 
-        for v in range(HALVES):
-            xs_picked = keep.tile([P, HALF], U8, name=f"xs_picked{v}", **byte_turn)
-            entries = offsets[:, v * (HALF // GROUP) : (v + 1) * (HALF // GROUP)]
-            nc.vector.tensor_copy(xs_picked[:], xs_table[:].indirect(entries))
+        def pick_scales(v):
+            lo, hi = parts[v]
+            xs_picked = keep.tile([P, hi - lo], U8, name=f"xs_picked{v}", **vector_turn)
+            nc.vector.tensor_copy(xs_picked[:], xs_table[:].indirect(offsets[:, lo // GROUP : hi // GROUP]))
             for r in range(QUAD // BLOCK_ROWS):
                 nc.sync.dma_start(xs_planes[v][r:P:QUAD, :].bitcast(I32), xs_picked[BLOCK_ROWS * r : P : QUAD, :].bitcast(I32))
 
-        w2_plane = keep.tile([P, N], U8, name="w2_plane", **byte_turn)
-        nc.gpsimd.memset(w2_plane[:].bitcast(I32), 0)
-        for q in range(P // QUAD):
-            nc.sync.dma_start(w2_plane[QUAD * q : QUAD * q + 4, :].bitcast(I32), w2_scales[0, 4 * q : 4 * q + 4, :].bitcast(I32))
+        pick_scales(0)
+        pick_scales(1)
 
         w1_bf = keep.tile([P, PACK, P, PACK], BF16, name="w1_bf", align_bytes=64)
         w1_dst = w1_bf[:].rearrange("p t m j -> p m t j")
-        for w1_part, rows in ((w1_head, slice(0, 1)), (w1_rest, slice(1, PACK))):
-            w1_src = w1_part[:].rearrange("p j (m t) -> p m t j", t=PACK)
-            nc.scalar.copy(w1_dst[:, 0:CAST_SPLIT, :, rows], w1_src[:, 0:CAST_SPLIT])
-            nc.vector.tensor_copy(w1_dst[:, CAST_SPLIT:P, :, rows], w1_src[:, CAST_SPLIT:P])
+        nc.scalar.copy(w1_dst[:, 0 : P // 2], w1_head[:].rearrange("p j (m t) -> p m t j", t=PACK))
+        nc.scalar.copy(w1_dst[:, P // 2 : P], w1_rest[:].rearrange("p j (m t) -> p m t j", t=PACK))
         w1_codes = keep.tile([P, H], U32, name="w1_codes", **vector_turn)
         w1_plane = keep.tile([P, H], U8, name="w1_plane", align_bytes=64)
         nc.vector.quantize_mx(out=w1_codes[:].bitcast(FP8X4), scales=w1_plane[:], in_=w1_bf[:].rearrange("p t m j -> p (t m j)"))
 
-        xw_picked = []
-        for u in range(UNITS):
-            words = keep.tile([P, UNIT], U32, name=f"xw_picked{u}", **vector_turn)
-            entries = offsets[:, u * (UNIT // GROUP) : (u + 1) * (UNIT // GROUP)]
-            nc.vector.tensor_copy(words[:], xw_table[:].indirect(entries))
-            xw_picked.append(words)
+        w2_plane = keep.tile([P, N], U8, name="w2_plane", **vector_turn)
+        nc.gpsimd.memset(w2_plane[:].bitcast(I32), 0)
+        for q in range(P // QUAD):
+            nc.sync.dma_start(w2_plane[QUAD * q : QUAD * q + 4, :].bitcast(I32), w2_scales[0, 4 * q : 4 * q + 4, :].bitcast(I32))
+
+        warm_bank = psum.tile([P, H], F32, name="warm_bank", tag="bank")
+        for width in WARM:
+            nc.tensor.matmul_mx(out=warm_bank[:, 0:width], lhsT=w1_codes[:, 0:P].bitcast(FP8X4), lhsT_scale=w1_plane[:, 0:P],
+                                rhs=w1_codes[:, 0:width].bitcast(FP8X4), rhs_scale=w1_plane[:, 0:width], start=True, stop=True)
 
         out_rows = out.rearrange("(a p) s -> p a s", p=P)
-        h_bf = [keep.tile([P, UNIT, PACK], BF16, name=f"h_bf{u}", align_bytes=64) for u in range(UNITS)]
+        xw_picked, h_bf, hidden, banks = {}, {}, {}, {}
+
+        def pick_words(u):
+            words = keep.tile([P, UNIT], U32, name=f"xw_picked{u}", **vector_turn)
+            nc.vector.tensor_copy(words[:], xw_table[:].indirect(offsets[:, u * (UNIT // GROUP) : (u + 1) * (UNIT // GROUP)]))
+            xw_picked[u] = words
 
         def first_layer(c):
             u, in_unit = divmod(c, UNIT // CHUNK)
-            v, in_half = divmod(c, HALF // CHUNK)
+            v = 0 if c * CHUNK < EARLY else 1
+            lo = c * CHUNK - parts[v][0]
             h_bank = psum.tile([P, PACK, CHUNK], F32, name="h_bank", tag="bank")
             for t in range(PACK):
                 nc.tensor.matmul_mx(
@@ -106,13 +109,22 @@ def tile_picked_phmlp_relu_p_kernel(tc, x_words, x_scales, w1, w2_words, w2_scal
                     lhsT=w1_codes[:, t * P : (t + 1) * P].bitcast(FP8X4),
                     lhsT_scale=w1_plane[:, t * P : (t + 1) * P],
                     rhs=xw_picked[u][:, in_unit * CHUNK : (in_unit + 1) * CHUNK].bitcast(FP8X4),
-                    rhs_scale=xs_planes[v][:, in_half * CHUNK : (in_half + 1) * CHUNK],
+                    rhs_scale=xs_planes[v][:, lo : lo + CHUNK],
                     start=True,
                     stop=True,
                 )
+            banks[c] = h_bank
+
+        def relu(c, on_vector):
+            u, in_unit = divmod(c, UNIT // CHUNK)
+            if u not in h_bf:
+                if on_vector:
+                    h_bf[u] = keep.tile([P, UNIT, PACK], BF16, name=f"h_bf{u}", **vector_turn)
+                else:
+                    h_bf[u] = keep.tile([P, UNIT, PACK], BF16, name=f"h_bf{u}", align_bytes=64)
             h_dst = h_bf[u][:, in_unit * CHUNK : (in_unit + 1) * CHUNK, :]
-            h_src = h_bank[:].rearrange("p t n -> p n t")
-            if c in VECTOR_RELU:
+            h_src = banks[c][:].rearrange("p t n -> p n t")
+            if on_vector:
                 nc.vector.tensor_scalar_max(h_dst, h_src, 0.0)
             else:
                 nc.scalar.activation(h_dst, h_src, RELU)
@@ -121,9 +133,10 @@ def tile_picked_phmlp_relu_p_kernel(tc, x_words, x_scales, w1, w2_words, w2_scal
             h_codes = keep.tile([P, UNIT], U32, name=f"h_codes{u}", **vector_turn)
             h_plane = keep.tile([P, UNIT], U8, name=f"h_plane{u}", align_bytes=64)
             nc.vector.quantize_mx(out=h_codes[:].bitcast(FP8X4), scales=h_plane[:], in_=h_bf[u][:].rearrange("p n t -> p (n t)"))
-            return h_codes, h_plane
+            hidden[u] = (h_codes, h_plane)
 
-        def second_pass(dst, a, h_codes, h_plane):
+        def second_pass(dst, a, u):
+            h_codes, h_plane = hidden[u]
             nc.tensor.matmul_mx(
                 out=dst,
                 lhsT=w2_codes[:, a * 2 * P : (a + 1) * 2 * P].bitcast(FP4X4),
@@ -134,33 +147,51 @@ def tile_picked_phmlp_relu_p_kernel(tc, x_words, x_scales, w1, w2_words, w2_scal
                 stop=True,
             )
 
-        for c in range(CHUNKS - 1):
-            first_layer(c)
-        hidden = [quantise_hidden(0)]
-        for u in range(UNITS):
-            if u + 1 < UNITS:
-                hidden.append(quantise_hidden(u + 1))
-            h_codes, h_plane = hidden[u]
-            if u == 0:
-                result = keep.tile([P, OUT_BLOCKS, UNIT], F32, name="result0", **vector_turn)
-            else:
-                result = keep.tile([P, OUT_BLOCKS, UNIT], F32, name=f"result{u}")
-            if u < FIRST_SHARED_UNIT:
-                out_bank = psum.tile([P, OUT_BLOCKS, UNIT], F32, name="out_bank", tag="bank")
-                for a in range(OUT_BLOCKS):
-                    second_pass(out_bank[:, a, :], a, h_codes, h_plane)
-                if u == 0:
-                    nc.vector.tensor_copy(result[:], out_bank[:])
-                else:
-                    nc.scalar.copy(result[:], out_bank[:])
-            else:
+        def second_layer(u, shared):
+            if shared:
+                pair = []
                 for a in range(OUT_BLOCKS):
                     block_bank = psum.tile([P, UNIT], F32, name="block_bank", tag="bank")
-                    second_pass(block_bank[:], a, h_codes, h_plane)
-                    if a == 0:
-                        nc.vector.tensor_copy(result[:, a, :], block_bank[:])
-                    else:
-                        nc.scalar.copy(result[:, a, :], block_bank[:])
+                    second_pass(block_bank[:], a, u)
+                    pair.append(block_bank)
+                banks["out", u] = pair
+            else:
+                out_bank = psum.tile([P, OUT_BLOCKS, UNIT], F32, name="out_bank", tag="bank")
+                for a in range(OUT_BLOCKS):
+                    second_pass(out_bank[:, a, :], a, u)
+                banks["out", u] = out_bank
+
+        def way_out(u, engine):
+            if engine == "scalar":
+                result = keep.tile([P, OUT_BLOCKS, UNIT], F32, name=f"result{u}")
+                nc.scalar.copy(result[:], banks["out", u][:])
+            else:
+                result = keep.tile([P, OUT_BLOCKS, UNIT], F32, name=f"result{u}", **vector_turn)
+                if engine == "vector":
+                    nc.vector.tensor_copy(result[:], banks["out", u][:])
+                else:
+                    nc.vector.tensor_copy(result[:, 1, :], banks["out", u][1][:])
+                    nc.scalar.copy(result[:, 0, :], banks["out", u][0][:])
             nc.sync.dma_start(out_rows[:, :, u * UNIT : (u + 1) * UNIT], result[:])
-            if u == 0:
-                first_layer(CHUNKS - 1)
+
+        for u in range(UNITS):
+            pick_words(u)
+        for c in range(7):
+            first_layer(c)
+        for c in range(4):
+            relu(c, c == 2)
+        quantise_hidden(0)
+        second_layer(0, False)
+        first_layer(7)
+        for c in range(4, 8):
+            relu(c, c == 4)
+        quantise_hidden(1)
+        second_layer(1, False)
+        quantise_hidden(2)
+        second_layer(2, False)
+        way_out(0, "vector")
+        quantise_hidden(3)
+        second_layer(3, True)
+        way_out(1, "scalar")
+        way_out(2, "vector")
+        way_out(3, "both")

@@ -27,7 +27,7 @@ CHUNK = 128
 UNITS, CHUNKS = S // UNIT, S // CHUNK
 OUT_BLOCKS = N // P
 EARLY = 512
-CAST_SPLIT = 64
+CAST_SPLIT = 88
 WARM = (512, 256)
 
 
@@ -38,7 +38,7 @@ def tile_picked_phmlp_relu_p_kernel(tc, x_words, x_scales, w1, w2_words, w2_scal
         psum = ctx.enter_context(tc.psum_pool(name="psum", bufs=BANKS))
 
         load_turn = dict(tag="load_turn", bufs=5, align_bytes=64)
-        vector_turn = dict(tag="vector_turn", bufs=20, align_bytes=64)
+        vector_turn = dict(tag="vector_turn", bufs=26, align_bytes=64)
 
         xs_table = keep.tile([P, T], U8, name="xs_table", align_bytes=64)
         nc.vector.memset(xs_table[:].bitcast(I32), 0)
@@ -50,13 +50,13 @@ def tile_picked_phmlp_relu_p_kernel(tc, x_words, x_scales, w1, w2_words, w2_scal
             xs_planes.append(xs_plane)
 
         w1_rows = w1.rearrange("(p j) c -> p j c", j=PACK)
-        w1_head = keep.tile([P, PACK, H // 2], F32, name="w1_head")
-        nc.sync.dma_start(w1_head[:], w1_rows[:, :, 0 : H // 2])
+        w1_head = keep.tile([P, 1, H], F32, name="w1_head")
+        nc.sync.dma_start(w1_head[:], w1_rows[:, 0:1, :])
         offsets = keep.tile([P, S // GROUP], U16, name="offsets")
         nc.sync.dma_start(offsets[:], offs)
         nc.sync.dma_start(xs_table[0:P:BLOCK_ROWS, :].bitcast(I32), x_scales[0].bitcast(I32))
-        w1_rest = keep.tile([P, PACK, H // 2], F32, name="w1_rest", **load_turn)
-        nc.sync.dma_start(w1_rest[:], w1_rows[:, :, H // 2 : H])
+        w1_rest = keep.tile([P, PACK - 1, H], F32, name="w1_rest", **load_turn)
+        nc.sync.dma_start(w1_rest[:], w1_rows[:, 1:PACK, :])
         xw_table = keep.tile([P, T], U32, name="xw_table", **load_turn)
         nc.sync.dma_start(xw_table[:].bitcast(I32), x_words[0].rearrange("p n t -> p (n t)").bitcast(I32))
         w2_codes = keep.tile([P, 2 * N], U8, name="w2_codes", **load_turn)
@@ -74,8 +74,10 @@ def tile_picked_phmlp_relu_p_kernel(tc, x_words, x_scales, w1, w2_words, w2_scal
 
         w1_bf = keep.tile([P, PACK, P, PACK], BF16, name="w1_bf", align_bytes=64)
         w1_dst = w1_bf[:].rearrange("p t m j -> p m t j")
-        nc.scalar.copy(w1_dst[:, 0 : P // 2], w1_head[:].rearrange("p j (m t) -> p m t j", t=PACK))
-        nc.scalar.copy(w1_dst[:, P // 2 : P], w1_rest[:].rearrange("p j (m t) -> p m t j", t=PACK))
+        for w1_part, rows in ((w1_head, slice(0, 1)), (w1_rest, slice(1, PACK))):
+            w1_src = w1_part[:].rearrange("p j (m t) -> p m t j", t=PACK)
+            nc.scalar.copy(w1_dst[:, 0:CAST_SPLIT, :, rows], w1_src[:, 0:CAST_SPLIT])
+            nc.vector.tensor_copy(w1_dst[:, CAST_SPLIT:P, :, rows], w1_src[:, CAST_SPLIT:P])
         w1_codes = keep.tile([P, H], U32, name="w1_codes", **vector_turn)
         w1_plane = keep.tile([P, H], U8, name="w1_plane", align_bytes=64)
         nc.vector.quantize_mx(out=w1_codes[:].bitcast(FP8X4), scales=w1_plane[:], in_=w1_bf[:].rearrange("p t m j -> p (t m j)"))
@@ -147,6 +149,41 @@ def tile_picked_phmlp_relu_p_kernel(tc, x_words, x_scales, w1, w2_words, w2_scal
                 stop=True,
             )
 
+        def quantise_chunk(c):
+            u, in_unit = divmod(c, UNIT // CHUNK)
+            h_codes = keep.tile([P, CHUNK], U32, name=f"hc_codes{c}", **vector_turn)
+            h_plane = keep.tile([P, CHUNK], U8, name=f"hc_plane{c}", align_bytes=64)
+            h_in = h_bf[u][:, in_unit * CHUNK : (in_unit + 1) * CHUNK, :].rearrange("p n t -> p (n t)")
+            nc.vector.quantize_mx(out=h_codes[:].bitcast(FP8X4), scales=h_plane[:], in_=h_in)
+            hidden["chunk", c] = (h_codes, h_plane)
+
+        def second_chunk(c, shared):
+            if shared:
+                pair = []
+                for a in range(OUT_BLOCKS):
+                    block_bank = psum.tile([P, CHUNK], F32, name="cblock_bank", tag="bank")
+                    second_pass(block_bank[:], a, ("chunk", c))
+                    pair.append(block_bank)
+                banks["cout", c] = pair
+            else:
+                out_bank = psum.tile([P, OUT_BLOCKS, CHUNK], F32, name="cout_bank", tag="bank")
+                for a in range(OUT_BLOCKS):
+                    second_pass(out_bank[:, a, :], a, ("chunk", c))
+                banks["cout", c] = out_bank
+
+        def way_out_chunk(c, engine):
+            if engine == "scalar":
+                result = keep.tile([P, OUT_BLOCKS, CHUNK], F32, name=f"cresult{c}")
+                nc.scalar.copy(result[:], banks["cout", c][:])
+            else:
+                result = keep.tile([P, OUT_BLOCKS, CHUNK], F32, name=f"cresult{c}", **vector_turn)
+                if engine == "vector":
+                    nc.vector.tensor_copy(result[:], banks["cout", c][:])
+                else:
+                    nc.vector.tensor_copy(result[:, 1, :], banks["cout", c][1][:])
+                    nc.scalar.copy(result[:, 0, :], banks["cout", c][0][:])
+            nc.sync.dma_start(out_rows[:, :, c * CHUNK : (c + 1) * CHUNK], result[:])
+
         def second_layer(u, shared):
             if shared:
                 pair = []
@@ -190,8 +227,11 @@ def tile_picked_phmlp_relu_p_kernel(tc, x_words, x_scales, w1, w2_words, w2_scal
         quantise_hidden(2)
         second_layer(2, False)
         way_out(0, "vector")
-        quantise_hidden(3)
-        second_layer(3, True)
+        quantise_chunk(6)
+        second_chunk(6, False)
+        quantise_chunk(7)
+        second_chunk(7, True)
         way_out(1, "scalar")
         way_out(2, "vector")
-        way_out(3, "both")
+        way_out_chunk(6, "scalar")
+        way_out_chunk(7, "both")

@@ -26,9 +26,9 @@ UNIT = 256
 CHUNK = 128
 UNITS, CHUNKS = S // UNIT, S // CHUNK
 OUT_BLOCKS = N // P
-EARLY = 512
-CAST_SPLIT = 88
-WARM = (512, 256)
+EARLY = 768
+CAST_SPLIT = 56
+WARM = (512, 512)
 
 
 def tile_picked_phmlp_relu_p_kernel(tc, x_words, x_scales, w1, w2_words, w2_scales, offs, out):
@@ -37,7 +37,7 @@ def tile_picked_phmlp_relu_p_kernel(tc, x_words, x_scales, w1, w2_words, w2_scal
         keep = ctx.enter_context(tc.tile_pool(name="keep", bufs=1))
         psum = ctx.enter_context(tc.psum_pool(name="psum", bufs=BANKS))
 
-        load_turn = dict(tag="load_turn", bufs=5, align_bytes=64)
+        load_turn = dict(tag="load_turn", bufs=6, align_bytes=64)
         vector_turn = dict(tag="vector_turn", bufs=26, align_bytes=64)
 
         xs_table = keep.tile([P, T], U8, name="xs_table", align_bytes=64)
@@ -57,6 +57,10 @@ def tile_picked_phmlp_relu_p_kernel(tc, x_words, x_scales, w1, w2_words, w2_scal
         nc.sync.dma_start(xs_table[0:P:BLOCK_ROWS, :].bitcast(I32), x_scales[0].bitcast(I32))
         w1_rest = keep.tile([P, PACK - 1, H], F32, name="w1_rest", **load_turn)
         nc.sync.dma_start(w1_rest[:], w1_rows[:, 1:PACK, :])
+        w2_plane = keep.tile([P, N], U8, name="w2_plane", **load_turn)
+        nc.vector.memset(w2_plane[:].bitcast(I32), 0)
+        for q in range(P // QUAD):
+            nc.sync.dma_start(w2_plane[QUAD * q : QUAD * q + 4, :].bitcast(I32), w2_scales[0, 4 * q : 4 * q + 4, :].bitcast(I32))
         xw_table = keep.tile([P, T], U32, name="xw_table", **load_turn)
         nc.sync.dma_start(xw_table[:].bitcast(I32), x_words[0].rearrange("p n t -> p (n t)").bitcast(I32))
         w2_codes = keep.tile([P, 2 * N], U8, name="w2_codes", **load_turn)
@@ -70,22 +74,21 @@ def tile_picked_phmlp_relu_p_kernel(tc, x_words, x_scales, w1, w2_words, w2_scal
                 nc.sync.dma_start(xs_planes[v][r:P:QUAD, :].bitcast(I32), xs_picked[BLOCK_ROWS * r : P : QUAD, :].bitcast(I32))
 
         pick_scales(0)
-        pick_scales(1)
 
         w1_bf = keep.tile([P, PACK, P, PACK], BF16, name="w1_bf", align_bytes=64)
         w1_dst = w1_bf[:].rearrange("p t m j -> p m t j")
-        for w1_part, rows in ((w1_head, slice(0, 1)), (w1_rest, slice(1, PACK))):
-            w1_src = w1_part[:].rearrange("p j (m t) -> p m t j", t=PACK)
-            nc.scalar.copy(w1_dst[:, 0:CAST_SPLIT, :, rows], w1_src[:, 0:CAST_SPLIT])
-            nc.vector.tensor_copy(w1_dst[:, CAST_SPLIT:P, :, rows], w1_src[:, CAST_SPLIT:P])
+        head_dst = w1_bf[:, :, :, 0].rearrange("p t (n e) -> p n t e", e=2)
+        head_src = w1_head[:, 0, :].rearrange("p (n e t) -> p n t e", e=2, t=PACK)
+        nc.scalar.copy(head_dst[:, 0 : CAST_SPLIT // 2], head_src[:, 0 : CAST_SPLIT // 2])
+        nc.vector.tensor_copy(head_dst[:, CAST_SPLIT // 2 : P // 2], head_src[:, CAST_SPLIT // 2 : P // 2])
+        w1_src = w1_rest[:].rearrange("p j (m t) -> p m t j", t=PACK)
+        nc.scalar.copy(w1_dst[:, 0:CAST_SPLIT, :, 1:PACK], w1_src[:, 0:CAST_SPLIT])
+        nc.vector.tensor_copy(w1_dst[:, CAST_SPLIT:P, :, 1:PACK], w1_src[:, CAST_SPLIT:P])
         w1_codes = keep.tile([P, H], U32, name="w1_codes", **vector_turn)
         w1_plane = keep.tile([P, H], U8, name="w1_plane", align_bytes=64)
         nc.vector.quantize_mx(out=w1_codes[:].bitcast(FP8X4), scales=w1_plane[:], in_=w1_bf[:].rearrange("p t m j -> p (t m j)"))
 
-        w2_plane = keep.tile([P, N], U8, name="w2_plane", **vector_turn)
-        nc.gpsimd.memset(w2_plane[:].bitcast(I32), 0)
-        for q in range(P // QUAD):
-            nc.sync.dma_start(w2_plane[QUAD * q : QUAD * q + 4, :].bitcast(I32), w2_scales[0, 4 * q : 4 * q + 4, :].bitcast(I32))
+        pick_scales(1)
 
         warm_bank = psum.tile([P, H], F32, name="warm_bank", tag="bank")
         for width in WARM:

@@ -227,14 +227,11 @@ def tile_picked_phmlp_relu_p_kernel(tc, x_words, x_scales, w1, w2_words, w2_scal
             relu(c, c == 4)
         quantise_hidden(1)
         second_layer(1, False)
-        quantise_hidden(2)
-        second_layer(2, False)
         way_out(0, "vector")
-        quantise_chunk(6)
-        second_chunk(6, False)
-        quantise_chunk(7)
-        second_chunk(7, True)
+        quantise_hidden(2)
+        second_layer(2, True)
+        quantise_hidden(3)
+        second_layer(3, True)
         way_out(1, "scalar")
-        way_out(2, "vector")
-        way_out_chunk(6, "scalar")
-        way_out_chunk(7, "both")
+        way_out(2, "both")
+        way_out(3, "both")

@@ -27,8 +27,7 @@ CHUNK = 128
 UNITS, CHUNKS = S // UNIT, S // CHUNK
 OUT_BLOCKS = N // P
 EARLY = 768
-CAST_SPLIT = 56
-WARM = (512, 512)
+WARM = (256, 256, 512, 256)
 
 
 def tile_picked_phmlp_relu_p_kernel(tc, x_words, x_scales, w1, w2_words, w2_scales, offs, out):
@@ -37,7 +36,7 @@ def tile_picked_phmlp_relu_p_kernel(tc, x_words, x_scales, w1, w2_words, w2_scal
         keep = ctx.enter_context(tc.tile_pool(name="keep", bufs=1))
         psum = ctx.enter_context(tc.psum_pool(name="psum", bufs=BANKS))
 
-        load_turn = dict(tag="load_turn", bufs=6, align_bytes=64)
+        load_turn = dict(tag="load_turn", bufs=5, align_bytes=64)
         vector_turn = dict(tag="vector_turn", bufs=26, align_bytes=64)
 
         xs_table = keep.tile([P, T], U8, name="xs_table", align_bytes=64)
@@ -59,12 +58,15 @@ def tile_picked_phmlp_relu_p_kernel(tc, x_words, x_scales, w1, w2_words, w2_scal
         nc.sync.dma_start(w1_rest[:], w1_rows[:, 1:PACK, :])
         w2_plane = keep.tile([P, N], U8, name="w2_plane", **load_turn)
         nc.vector.memset(w2_plane[:].bitcast(I32), 0)
-        for q in range(P // QUAD):
+
+        def load_w2_scales(q):
             nc.sync.dma_start(w2_plane[QUAD * q : QUAD * q + 4, :].bitcast(I32), w2_scales[0, 4 * q : 4 * q + 4, :].bitcast(I32))
+
+        load_w2_scales(0)
         xw_table = keep.tile([P, T], U32, name="xw_table", **load_turn)
         nc.sync.dma_start(xw_table[:].bitcast(I32), x_words[0].rearrange("p n t -> p (n t)").bitcast(I32))
-        w2_codes = keep.tile([P, 2 * N], U8, name="w2_codes", **load_turn)
-        nc.sync.dma_start(w2_codes[:].bitcast(I32), w2_words[0].bitcast(I32))
+        for q in range(1, P // QUAD):
+            load_w2_scales(q)
 
         def pick_scales(v):
             lo, hi = parts[v]
@@ -79,14 +81,20 @@ def tile_picked_phmlp_relu_p_kernel(tc, x_words, x_scales, w1, w2_words, w2_scal
         w1_dst = w1_bf[:].rearrange("p t m j -> p m t j")
         head_dst = w1_bf[:, :, :, 0].rearrange("p t (n e) -> p n t e", e=2)
         head_src = w1_head[:, 0, :].rearrange("p (n e t) -> p n t e", e=2, t=PACK)
-        nc.scalar.copy(head_dst[:, 0 : CAST_SPLIT // 2], head_src[:, 0 : CAST_SPLIT // 2])
-        nc.vector.tensor_copy(head_dst[:, CAST_SPLIT // 2 : P // 2], head_src[:, CAST_SPLIT // 2 : P // 2])
+        nc.vector.tensor_copy(head_dst[:, :, 0:2], head_src[:, :, 0:2])
+        nc.scalar.copy(head_dst[:, :, 2:PACK], head_src[:, :, 2:PACK])
         w1_src = w1_rest[:].rearrange("p j (m t) -> p m t j", t=PACK)
-        nc.scalar.copy(w1_dst[:, 0:CAST_SPLIT, :, 1:PACK], w1_src[:, 0:CAST_SPLIT])
-        nc.vector.tensor_copy(w1_dst[:, CAST_SPLIT:P, :, 1:PACK], w1_src[:, CAST_SPLIT:P])
+        nc.vector.tensor_copy(w1_dst[:, :, 0:2, 1:PACK], w1_src[:, :, 0:2])
+        nc.scalar.copy(w1_dst[:, :, 2:PACK, 1:PACK], w1_src[:, :, 2:PACK])
         w1_codes = keep.tile([P, H], U32, name="w1_codes", **vector_turn)
         w1_plane = keep.tile([P, H], U8, name="w1_plane", align_bytes=64)
-        nc.vector.quantize_mx(out=w1_codes[:].bitcast(FP8X4), scales=w1_plane[:], in_=w1_bf[:].rearrange("p t m j -> p (t m j)"))
+        for t in range(0, PACK, 2):
+            cols = slice(t * P, (t + 2) * P)
+            w1_in = w1_bf[:, t : t + 2].rearrange("p t m j -> p (t m j)")
+            nc.vector.quantize_mx(out=w1_codes[:, cols].bitcast(FP8X4), scales=w1_plane[:, cols], in_=w1_in)
+
+        w2_codes = keep.tile([P, 2 * N], U8, name="w2_codes", **vector_turn)
+        nc.sync.dma_start(w2_codes[:].bitcast(I32), w2_words[0].bitcast(I32))
 
         pick_scales(1)
 

@@ -22,12 +22,16 @@ GROUP = 16
 BLOCK_ROWS = 8
 BANKS = 8
 
+HALF = 512
 UNIT = 256
 CHUNK = 128
-UNITS, CHUNKS = S // UNIT, S // CHUNK
+HALVES, UNITS, CHUNKS = S // HALF, S // UNIT, S // CHUNK
+PER_UNIT = UNIT // CHUNK
 OUT_BLOCKS = N // P
-EARLY = 768
-WARM = (256, 256, 512, 256)
+PAIR = 2
+WARM_UP_PASSES = 4
+
+VECTOR_RELU = (2, 4)
 
 
 def tile_picked_phmlp_relu_p_kernel(tc, x_words, x_scales, w1, w2_words, w2_scales, offs, out):
@@ -36,15 +40,15 @@ def tile_picked_phmlp_relu_p_kernel(tc, x_words, x_scales, w1, w2_words, w2_scal
         keep = ctx.enter_context(tc.tile_pool(name="keep", bufs=1))
         psum = ctx.enter_context(tc.psum_pool(name="psum", bufs=BANKS))
 
-        load_turn = dict(tag="load_turn", bufs=5, align_bytes=64)
-        vector_turn = dict(tag="vector_turn", bufs=26, align_bytes=64)
+        load_turn = dict(tag="load_turn", bufs=HALVES + 2, align_bytes=64)
+        vector_slots = HALVES + PACK // PAIR + 2 + UNITS + len(VECTOR_RELU) + UNITS + (UNITS - 1)
+        vector_turn = dict(tag="vector_turn", bufs=vector_slots, align_bytes=64)
 
         xs_table = keep.tile([P, T], U8, name="xs_table", align_bytes=64)
         nc.vector.memset(xs_table[:].bitcast(I32), 0)
-        parts = ((0, EARLY), (EARLY, S))
         xs_planes = []
-        for v, (lo, hi) in enumerate(parts):
-            xs_plane = keep.tile([P, hi - lo], U8, name=f"xs_plane{v}", **load_turn)
+        for v in range(HALVES):
+            xs_plane = keep.tile([P, HALF], U8, name=f"xs_plane{v}", **load_turn)
             nc.vector.memset(xs_plane[:].bitcast(I32), 0)
             xs_planes.append(xs_plane)
 
@@ -56,190 +60,146 @@ def tile_picked_phmlp_relu_p_kernel(tc, x_words, x_scales, w1, w2_words, w2_scal
         nc.sync.dma_start(xs_table[0:P:BLOCK_ROWS, :].bitcast(I32), x_scales[0].bitcast(I32))
         w1_rest = keep.tile([P, PACK - 1, H], F32, name="w1_rest", **load_turn)
         nc.sync.dma_start(w1_rest[:], w1_rows[:, 1:PACK, :])
-        w2_plane = keep.tile([P, N], U8, name="w2_plane", **load_turn)
-        nc.vector.memset(w2_plane[:].bitcast(I32), 0)
-
-        def load_w2_scales(q):
-            nc.sync.dma_start(w2_plane[QUAD * q : QUAD * q + 4, :].bitcast(I32), w2_scales[0, 4 * q : 4 * q + 4, :].bitcast(I32))
-
-        load_w2_scales(0)
         xw_table = keep.tile([P, T], U32, name="xw_table", **load_turn)
         nc.sync.dma_start(xw_table[:].bitcast(I32), x_words[0].rearrange("p n t -> p (n t)").bitcast(I32))
-        for q in range(1, P // QUAD):
-            load_w2_scales(q)
 
-        def pick_scales(v):
-            lo, hi = parts[v]
-            xs_picked = keep.tile([P, hi - lo], U8, name=f"xs_picked{v}", **vector_turn)
-            nc.vector.tensor_copy(xs_picked[:], xs_table[:].indirect(offsets[:, lo // GROUP : hi // GROUP]))
-            for r in range(QUAD // BLOCK_ROWS):
+        for v in range(HALVES):
+            xs_picked = keep.tile([P, HALF], U8, name=f"xs_picked{v}", **vector_turn)
+            entries = offsets[:, v * (HALF // GROUP) : (v + 1) * (HALF // GROUP)]
+            nc.vector.tensor_copy(xs_picked[:], xs_table[:].indirect(entries))
+            for r in range(PACK):
                 nc.sync.dma_start(xs_planes[v][r:P:QUAD, :].bitcast(I32), xs_picked[BLOCK_ROWS * r : P : QUAD, :].bitcast(I32))
 
-        pick_scales(0)
-
         w1_bf = keep.tile([P, PACK, P, PACK], BF16, name="w1_bf", align_bytes=64)
-        w1_dst = w1_bf[:].rearrange("p t m j -> p m t j")
         head_dst = w1_bf[:, :, :, 0].rearrange("p t (n e) -> p n t e", e=2)
         head_src = w1_head[:, 0, :].rearrange("p (n e t) -> p n t e", e=2, t=PACK)
-        nc.vector.tensor_copy(head_dst[:, :, 0:2], head_src[:, :, 0:2])
-        nc.scalar.copy(head_dst[:, :, 2:PACK], head_src[:, :, 2:PACK])
-        w1_src = w1_rest[:].rearrange("p j (m t) -> p m t j", t=PACK)
-        nc.vector.tensor_copy(w1_dst[:, :, 0:2, 1:PACK], w1_src[:, :, 0:2])
-        nc.scalar.copy(w1_dst[:, :, 2:PACK, 1:PACK], w1_src[:, :, 2:PACK])
-        w1_codes = keep.tile([P, H], U32, name="w1_codes", **vector_turn)
-        w1_plane = keep.tile([P, H], U8, name="w1_plane", align_bytes=64)
-        for t in range(0, PACK, 2):
-            cols = slice(t * P, (t + 2) * P)
-            w1_in = w1_bf[:, t : t + 2].rearrange("p t m j -> p (t m j)")
-            nc.vector.quantize_mx(out=w1_codes[:, cols].bitcast(FP8X4), scales=w1_plane[:, cols], in_=w1_in)
+        nc.vector.tensor_copy(head_dst[:, :, 0:PAIR], head_src[:, :, 0:PAIR])
+        nc.scalar.copy(head_dst[:, :, PAIR:PACK], head_src[:, :, PAIR:PACK])
+        rest_dst = w1_bf[:].rearrange("p t m j -> p m t j")
+        rest_src = w1_rest[:].rearrange("p j (m t) -> p m t j", t=PACK)
+        nc.vector.tensor_copy(rest_dst[:, :, 0:PAIR, 1:PACK], rest_src[:, :, 0:PAIR])
+        nc.scalar.copy(rest_dst[:, :, PAIR:PACK, 1:PACK], rest_src[:, :, PAIR:PACK])
+
+        w1_pairs = {}
+        for first_tile in (PAIR, 0):
+            pair_codes = keep.tile([P, PAIR * P], U32, name=f"w1_codes{first_tile}", **vector_turn)
+            pair_plane = keep.tile([P, PAIR * P], U8, name=f"w1_plane{first_tile}", align_bytes=64)
+            pair_bf = w1_bf[:, first_tile : first_tile + PAIR].rearrange("p t m j -> p (t m j)")
+            nc.vector.quantize_mx(out=pair_codes[:].bitcast(FP8X4), scales=pair_plane[:], in_=pair_bf)
+            w1_pairs[first_tile] = (pair_codes, pair_plane)
 
         w2_codes = keep.tile([P, 2 * N], U8, name="w2_codes", **vector_turn)
         nc.sync.dma_start(w2_codes[:].bitcast(I32), w2_words[0].bitcast(I32))
+        w2_plane = keep.tile([P, N], U8, name="w2_plane", **vector_turn)
+        nc.vector.memset(w2_plane[:].bitcast(I32), 0)
+        for q in range(P // QUAD):
+            w2_rows = w2_scales[0, PACK * q : PACK * (q + 1), :]
+            nc.sync.dma_start(w2_plane[QUAD * q : QUAD * q + PACK, :].bitcast(I32), w2_rows.bitcast(I32))
 
-        pick_scales(1)
-
+        warm_codes, warm_plane = w1_pairs[PAIR]
         warm_bank = psum.tile([P, H], F32, name="warm_bank", tag="bank")
-        for width in WARM:
-            nc.tensor.matmul_mx(out=warm_bank[:, 0:width], lhsT=w1_codes[:, 0:P].bitcast(FP8X4), lhsT_scale=w1_plane[:, 0:P],
-                                rhs=w1_codes[:, 0:width].bitcast(FP8X4), rhs_scale=w1_plane[:, 0:width], start=True, stop=True)
-
-        out_rows = out.rearrange("(a p) s -> p a s", p=P)
-        xw_picked, h_bf, hidden, banks = {}, {}, {}, {}
-
-        def pick_words(u):
-            words = keep.tile([P, UNIT], U32, name=f"xw_picked{u}", **vector_turn)
-            nc.vector.tensor_copy(words[:], xw_table[:].indirect(offsets[:, u * (UNIT // GROUP) : (u + 1) * (UNIT // GROUP)]))
-            xw_picked[u] = words
-
-        def first_layer(c):
-            u, in_unit = divmod(c, UNIT // CHUNK)
-            v = 0 if c * CHUNK < EARLY else 1
-            lo = c * CHUNK - parts[v][0]
-            h_bank = psum.tile([P, PACK, CHUNK], F32, name="h_bank", tag="bank")
-            for t in range(PACK):
-                nc.tensor.matmul_mx(
-                    out=h_bank[:, t, :],
-                    lhsT=w1_codes[:, t * P : (t + 1) * P].bitcast(FP8X4),
-                    lhsT_scale=w1_plane[:, t * P : (t + 1) * P],
-                    rhs=xw_picked[u][:, in_unit * CHUNK : (in_unit + 1) * CHUNK].bitcast(FP8X4),
-                    rhs_scale=xs_planes[v][:, lo : lo + CHUNK],
-                    start=True,
-                    stop=True,
-                )
-            banks[c] = h_bank
-
-        def relu(c, on_vector):
-            u, in_unit = divmod(c, UNIT // CHUNK)
-            if u not in h_bf:
-                if on_vector:
-                    h_bf[u] = keep.tile([P, UNIT, PACK], BF16, name=f"h_bf{u}", **vector_turn)
-                else:
-                    h_bf[u] = keep.tile([P, UNIT, PACK], BF16, name=f"h_bf{u}", align_bytes=64)
-            h_dst = h_bf[u][:, in_unit * CHUNK : (in_unit + 1) * CHUNK, :]
-            h_src = banks[c][:].rearrange("p t n -> p n t")
-            if on_vector:
-                nc.vector.tensor_scalar_max(h_dst, h_src, 0.0)
-            else:
-                nc.scalar.activation(h_dst, h_src, RELU)
-
-        def quantise_hidden(u):
-            h_codes = keep.tile([P, UNIT], U32, name=f"h_codes{u}", **vector_turn)
-            h_plane = keep.tile([P, UNIT], U8, name=f"h_plane{u}", align_bytes=64)
-            nc.vector.quantize_mx(out=h_codes[:].bitcast(FP8X4), scales=h_plane[:], in_=h_bf[u][:].rearrange("p n t -> p (n t)"))
-            hidden[u] = (h_codes, h_plane)
-
-        def second_pass(dst, a, u):
-            h_codes, h_plane = hidden[u]
+        for warm_pass in range(WARM_UP_PASSES):
             nc.tensor.matmul_mx(
-                out=dst,
-                lhsT=w2_codes[:, a * 2 * P : (a + 1) * 2 * P].bitcast(FP4X4),
-                lhsT_scale=w2_plane[:, a * P : (a + 1) * P],
-                rhs=h_codes[:].bitcast(FP8X4),
-                rhs_scale=h_plane[:],
+                out=warm_bank[:, 0 : PAIR * P],
+                lhsT=warm_codes[:, 0:P].bitcast(FP8X4),
+                lhsT_scale=warm_plane[:, 0:P],
+                rhs=warm_codes[:].bitcast(FP8X4),
+                rhs_scale=warm_plane[:],
                 start=True,
                 stop=True,
             )
 
-        def quantise_chunk(c):
-            u, in_unit = divmod(c, UNIT // CHUNK)
-            h_codes = keep.tile([P, CHUNK], U32, name=f"hc_codes{c}", **vector_turn)
-            h_plane = keep.tile([P, CHUNK], U8, name=f"hc_plane{c}", align_bytes=64)
-            h_in = h_bf[u][:, in_unit * CHUNK : (in_unit + 1) * CHUNK, :].rearrange("p n t -> p (n t)")
-            nc.vector.quantize_mx(out=h_codes[:].bitcast(FP8X4), scales=h_plane[:], in_=h_in)
-            hidden["chunk", c] = (h_codes, h_plane)
+        xw_picked = []
+        for u in range(UNITS):
+            words = keep.tile([P, UNIT], U32, name=f"xw_picked{u}", **vector_turn)
+            entries = offsets[:, u * (UNIT // GROUP) : (u + 1) * (UNIT // GROUP)]
+            nc.vector.tensor_copy(words[:], xw_table[:].indirect(entries))
+            xw_picked.append(words)
 
-        def second_chunk(c, shared):
-            if shared:
-                pair = []
-                for a in range(OUT_BLOCKS):
-                    block_bank = psum.tile([P, CHUNK], F32, name="cblock_bank", tag="bank")
-                    second_pass(block_bank[:], a, ("chunk", c))
-                    pair.append(block_bank)
-                banks["cout", c] = pair
+        out_rows = out.rearrange("(a p) s -> p a s", p=P)
+        h_banks, h_bf, out_banks = {}, {}, {}
+
+        def first_layer(c):
+            u, in_unit = divmod(c, PER_UNIT)
+            v, in_half = divmod(c, HALF // CHUNK)
+            h_bank = psum.tile([P, PACK, CHUNK], F32, name="h_bank", tag="bank")
+            for t in range(PACK):
+                pair_codes, pair_plane = w1_pairs[t - t % PAIR]
+                columns = slice(t % PAIR * P, (t % PAIR + 1) * P)
+                nc.tensor.matmul_mx(
+                    out=h_bank[:, t, :],
+                    lhsT=pair_codes[:, columns].bitcast(FP8X4),
+                    lhsT_scale=pair_plane[:, columns],
+                    rhs=xw_picked[u][:, in_unit * CHUNK : (in_unit + 1) * CHUNK].bitcast(FP8X4),
+                    rhs_scale=xs_planes[v][:, in_half * CHUNK : (in_half + 1) * CHUNK],
+                    start=True,
+                    stop=True,
+                )
+            h_banks[c] = h_bank
+
+        def relu(c):
+            u, in_unit = divmod(c, PER_UNIT)
+            if in_unit == 0:
+                placing = vector_turn if c in VECTOR_RELU else dict(align_bytes=64)
+                h_bf[u] = keep.tile([P, UNIT, PACK], BF16, name=f"h_bf{u}", **placing)
+            h_dst = h_bf[u][:, in_unit * CHUNK : (in_unit + 1) * CHUNK, :]
+            h_src = h_banks[c][:].rearrange("p t n -> p n t")
+            if c in VECTOR_RELU:
+                nc.vector.tensor_scalar_max(h_dst, h_src, 0.0)
             else:
-                out_bank = psum.tile([P, OUT_BLOCKS, CHUNK], F32, name="cout_bank", tag="bank")
-                for a in range(OUT_BLOCKS):
-                    second_pass(out_bank[:, a, :], a, ("chunk", c))
-                banks["cout", c] = out_bank
+                nc.scalar.activation(h_dst, h_src, RELU)
 
-        def way_out_chunk(c, engine):
-            if engine == "scalar":
-                result = keep.tile([P, OUT_BLOCKS, CHUNK], F32, name=f"cresult{c}")
-                nc.scalar.copy(result[:], banks["cout", c][:])
-            else:
-                result = keep.tile([P, OUT_BLOCKS, CHUNK], F32, name=f"cresult{c}", **vector_turn)
-                if engine == "vector":
-                    nc.vector.tensor_copy(result[:], banks["cout", c][:])
-                else:
-                    nc.vector.tensor_copy(result[:, 1, :], banks["cout", c][1][:])
-                    nc.scalar.copy(result[:, 0, :], banks["cout", c][0][:])
-            nc.sync.dma_start(out_rows[:, :, c * CHUNK : (c + 1) * CHUNK], result[:])
+        def second_layer(u, bank_each):
+            h_codes = keep.tile([P, UNIT], U32, name=f"h_codes{u}", **vector_turn)
+            h_plane = keep.tile([P, UNIT], U8, name=f"h_plane{u}", align_bytes=64)
+            nc.vector.quantize_mx(out=h_codes[:].bitcast(FP8X4), scales=h_plane[:], in_=h_bf[u][:].rearrange("p n t -> p (n t)"))
 
-        def second_layer(u, shared):
-            if shared:
-                pair = []
+            def product(dst, a):
+                nc.tensor.matmul_mx(
+                    out=dst,
+                    lhsT=w2_codes[:, a * 2 * P : (a + 1) * 2 * P].bitcast(FP4X4),
+                    lhsT_scale=w2_plane[:, a * P : (a + 1) * P],
+                    rhs=h_codes[:].bitcast(FP8X4),
+                    rhs_scale=h_plane[:],
+                    start=True,
+                    stop=True,
+                )
+
+            if bank_each:
+                out_banks[u] = []
                 for a in range(OUT_BLOCKS):
                     block_bank = psum.tile([P, UNIT], F32, name="block_bank", tag="bank")
-                    second_pass(block_bank[:], a, u)
-                    pair.append(block_bank)
-                banks["out", u] = pair
+                    product(block_bank[:], a)
+                    out_banks[u].append(block_bank)
             else:
                 out_bank = psum.tile([P, OUT_BLOCKS, UNIT], F32, name="out_bank", tag="bank")
                 for a in range(OUT_BLOCKS):
-                    second_pass(out_bank[:, a, :], a, u)
-                banks["out", u] = out_bank
+                    product(out_bank[:, a, :], a)
+                out_banks[u] = out_bank
 
-        def way_out(u, engine):
-            if engine == "scalar":
-                result = keep.tile([P, OUT_BLOCKS, UNIT], F32, name=f"result{u}")
-                nc.scalar.copy(result[:], banks["out", u][:])
-            else:
-                result = keep.tile([P, OUT_BLOCKS, UNIT], F32, name=f"result{u}", **vector_turn)
-                if engine == "vector":
-                    nc.vector.tensor_copy(result[:], banks["out", u][:])
-                else:
-                    nc.vector.tensor_copy(result[:, 1, :], banks["out", u][1][:])
-                    nc.scalar.copy(result[:, 0, :], banks["out", u][0][:])
+        def store(u, result):
             nc.sync.dma_start(out_rows[:, :, u * UNIT : (u + 1) * UNIT], result[:])
 
-        for u in range(UNITS):
-            pick_words(u)
-        for c in range(7):
+        for c in range(CHUNKS):
             first_layer(c)
-        for c in range(4):
-            relu(c, c == 2)
-        quantise_hidden(0)
-        second_layer(0, False)
-        first_layer(7)
-        for c in range(4, 8):
-            relu(c, c == 4)
-        quantise_hidden(1)
-        second_layer(1, False)
-        way_out(0, "vector")
-        quantise_hidden(2)
-        second_layer(2, True)
-        quantise_hidden(3)
-        second_layer(3, True)
-        way_out(1, "scalar")
-        way_out(2, "both")
-        way_out(3, "both")
+            if c < 2 * PER_UNIT:
+                relu(c)
+        second_layer(0, bank_each=False)
+        for c in range(2 * PER_UNIT, CHUNKS):
+            relu(c)
+        second_layer(1, bank_each=False)
+
+        result0 = keep.tile([P, OUT_BLOCKS, UNIT], F32, name="result0", **vector_turn)
+        nc.vector.tensor_copy(result0[:], out_banks[0][:])
+        store(0, result0)
+        for u in range(2, UNITS):
+            second_layer(u, bank_each=True)
+
+        result1 = keep.tile([P, OUT_BLOCKS, UNIT], F32, name="result1")
+        nc.scalar.copy(result1[:], out_banks[1][:])
+        store(1, result1)
+        for u in range(2, UNITS):
+            result = keep.tile([P, OUT_BLOCKS, UNIT], F32, name=f"result{u}", **vector_turn)
+            nc.vector.tensor_copy(result[:, 1, :], out_banks[u][1][:])
+            nc.scalar.copy(result[:, 0, :], out_banks[u][0][:])
+            store(u, result)

@@ -22,14 +22,15 @@ GROUP = 16
 BLOCK_ROWS = 8
 BANKS = 8
 
-HALF = 512
+FIRST = 736
 UNIT = 256
 CHUNK = 128
-HALVES, UNITS, CHUNKS = S // HALF, S // UNIT, S // CHUNK
+UNITS, CHUNKS = S // UNIT, S // CHUNK
 PER_UNIT = UNIT // CHUNK
 OUT_BLOCKS = N // P
 PAIR = 2
 WARM_UP_PASSES = 4
+CAST_SPLIT = 64
 
 VECTOR_RELU = (2, 4)
 
@@ -40,17 +41,16 @@ def tile_picked_phmlp_relu_p_kernel(tc, x_words, x_scales, w1, w2_words, w2_scal
         keep = ctx.enter_context(tc.tile_pool(name="keep", bufs=1))
         psum = ctx.enter_context(tc.psum_pool(name="psum", bufs=BANKS))
 
-        load_turn = dict(tag="load_turn", bufs=HALVES + 2, align_bytes=64)
-        vector_slots = HALVES + PACK // PAIR + 2 + UNITS + len(VECTOR_RELU) + UNITS + (UNITS - 1)
+        load_turn = dict(tag="load_turn", bufs=1 + 2, align_bytes=64)
+        vector_slots = 2 + PACK // PAIR + 1 + UNITS + len(VECTOR_RELU) + UNITS + (UNITS - 1)
         vector_turn = dict(tag="vector_turn", bufs=vector_slots, align_bytes=64)
 
         xs_table = keep.tile([P, T], U8, name="xs_table", align_bytes=64)
         nc.vector.memset(xs_table[:].bitcast(I32), 0)
-        xs_planes = []
-        for v in range(HALVES):
-            xs_plane = keep.tile([P, HALF], U8, name=f"xs_plane{v}", **load_turn)
-            nc.vector.memset(xs_plane[:].bitcast(I32), 0)
-            xs_planes.append(xs_plane)
+        w2_plane = keep.tile([P, N], U8, name="w2_plane", align_bytes=64)
+        nc.vector.memset(w2_plane[:].bitcast(I32), 0)
+        xs_plane = keep.tile([P, S], U8, name="xs_plane", **load_turn)
+        nc.vector.memset(xs_plane[:].bitcast(I32), 0)
 
         w1_rows = w1.rearrange("(p j) c -> p j c", j=PACK)
         w1_head = keep.tile([P, 1, H], F32, name="w1_head")
@@ -60,51 +60,68 @@ def tile_picked_phmlp_relu_p_kernel(tc, x_words, x_scales, w1, w2_words, w2_scal
         nc.sync.dma_start(xs_table[0:P:BLOCK_ROWS, :].bitcast(I32), x_scales[0].bitcast(I32))
         w1_rest = keep.tile([P, PACK - 1, H], F32, name="w1_rest", **load_turn)
         nc.sync.dma_start(w1_rest[:], w1_rows[:, 1:PACK, :])
-        xw_table = keep.tile([P, T], U32, name="xw_table", **load_turn)
-        nc.sync.dma_start(xw_table[:].bitcast(I32), x_words[0].rearrange("p n t -> p (n t)").bitcast(I32))
 
-        for v in range(HALVES):
-            xs_picked = keep.tile([P, HALF], U8, name=f"xs_picked{v}", **vector_turn)
-            entries = offsets[:, v * (HALF // GROUP) : (v + 1) * (HALF // GROUP)]
-            nc.vector.tensor_copy(xs_picked[:], xs_table[:].indirect(entries))
-            for r in range(PACK):
-                nc.sync.dma_start(xs_planes[v][r:P:QUAD, :].bitcast(I32), xs_picked[BLOCK_ROWS * r : P : QUAD, :].bitcast(I32))
-
-        w1_bf = keep.tile([P, PACK, P, PACK], BF16, name="w1_bf", align_bytes=64)
-        head_dst = w1_bf[:, :, :, 0].rearrange("p t (n e) -> p n t e", e=2)
-        head_src = w1_head[:, 0, :].rearrange("p (n e t) -> p n t e", e=2, t=PACK)
-        nc.vector.tensor_copy(head_dst[:, :, 0:PAIR], head_src[:, :, 0:PAIR])
-        nc.scalar.copy(head_dst[:, :, PAIR:PACK], head_src[:, :, PAIR:PACK])
-        rest_dst = w1_bf[:].rearrange("p t m j -> p m t j")
-        rest_src = w1_rest[:].rearrange("p j (m t) -> p m t j", t=PACK)
-        nc.vector.tensor_copy(rest_dst[:, :, 0:PAIR, 1:PACK], rest_src[:, :, 0:PAIR])
-        nc.scalar.copy(rest_dst[:, :, PAIR:PACK, 1:PACK], rest_src[:, :, PAIR:PACK])
-
-        w1_pairs = {}
-        for first_tile in (PAIR, 0):
-            pair_codes = keep.tile([P, PAIR * P], U32, name=f"w1_codes{first_tile}", **vector_turn)
-            pair_plane = keep.tile([P, PAIR * P], U8, name=f"w1_plane{first_tile}", align_bytes=64)
-            pair_bf = w1_bf[:, first_tile : first_tile + PAIR].rearrange("p t m j -> p (t m j)")
-            nc.vector.quantize_mx(out=pair_codes[:].bitcast(FP8X4), scales=pair_plane[:], in_=pair_bf)
-            w1_pairs[first_tile] = (pair_codes, pair_plane)
-
-        w2_codes = keep.tile([P, 2 * N], U8, name="w2_codes", **vector_turn)
-        nc.sync.dma_start(w2_codes[:].bitcast(I32), w2_words[0].bitcast(I32))
-        w2_plane = keep.tile([P, N], U8, name="w2_plane", **vector_turn)
-        nc.vector.memset(w2_plane[:].bitcast(I32), 0)
-        for q in range(P // QUAD):
+        def load_w2_scales(q):
             w2_rows = w2_scales[0, PACK * q : PACK * (q + 1), :]
             nc.sync.dma_start(w2_plane[QUAD * q : QUAD * q + PACK, :].bitcast(I32), w2_rows.bitcast(I32))
 
+        for q in range(P // QUAD - 1):
+            load_w2_scales(q)
+        xw_table = keep.tile([P, T], U32, name="xw_table", **load_turn)
+        nc.sync.dma_start(xw_table[:].bitcast(I32), x_words[0].rearrange("p n t -> p (n t)").bitcast(I32))
+        load_w2_scales(P // QUAD - 1)
+
+        def pick_scales(lo, hi):
+            picked = keep.tile([P, hi - lo], U8, name=f"xs_picked{lo}", **vector_turn)
+            nc.vector.tensor_copy(picked[:], xs_table[:].indirect(offsets[:, lo // GROUP : hi // GROUP]))
+            for r in range(PACK):
+                nc.sync.dma_start(xs_plane[r:P:QUAD, lo:hi].bitcast(I32), picked[BLOCK_ROWS * r : P : QUAD, :].bitcast(I32))
+            return picked
+
+        first_picked = pick_scales(0, FIRST)
+
+        w1_bf = {first_tile: keep.tile([P, PAIR, P, PACK], BF16, name=f"w1_bf{first_tile}", align_bytes=64) for first_tile in (PAIR, 0)}
+        head_src = w1_head[:, 0, :].rearrange("p (n e t) -> p n t e", e=2, t=PACK)
+        rest_src = w1_rest[:].rearrange("p j (m t) -> p m t j", t=PACK)
+        shares = (
+            (nc.vector.tensor_copy, PAIR, 0, CAST_SPLIT),
+            (nc.scalar.copy, PAIR, CAST_SPLIT, P),
+            (nc.scalar.copy, 0, 0, P),
+        )
+        for cast, first_tile, lo, hi in shares:
+            head_dst = w1_bf[first_tile][:, :, :, 0].rearrange("p t (n e) -> p n t e", e=2)
+            cast(head_dst[:, lo // 2 : hi // 2], head_src[:, lo // 2 : hi // 2, first_tile : first_tile + PAIR])
+        for cast, first_tile, lo, hi in shares:
+            rest_dst = w1_bf[first_tile][:].rearrange("p t m j -> p m t j")
+            cast(rest_dst[:, lo:hi, :, 1:PACK], rest_src[:, lo:hi, first_tile : first_tile + PAIR])
+
+        w1_pairs = {}
+        w1_codes = keep.tile([P, PACK * P], U32, name="w1_codes", align_bytes=64)
+
+        def quantise_pair(first_tile):
+            pair_codes = w1_codes[:, first_tile * P : (first_tile + PAIR) * P]
+            pair_plane = keep.tile([P, PAIR * P], U8, name=f"w1_plane{first_tile}", **vector_turn)
+            pair_bf = w1_bf[first_tile][:].rearrange("p t m j -> p (t m j)")
+            nc.vector.quantize_mx(out=pair_codes.bitcast(FP8X4), scales=pair_plane[:], in_=pair_bf)
+            w1_pairs[first_tile] = (pair_codes, pair_plane)
+
+        quantise_pair(PAIR)
+        pick_scales(FIRST, S)
+        quantise_pair(0)
+
+        w2_codes = keep.tile([P, 2 * N], U8, name="w2_codes", **vector_turn)
+        nc.sync.dma_start(w2_codes[:].bitcast(I32), w2_words[0].bitcast(I32))
+
         warm_codes, warm_plane = w1_pairs[PAIR]
         warm_bank = psum.tile([P, H], F32, name="warm_bank", tag="bank")
-        for warm_pass in range(WARM_UP_PASSES):
+        warm_moving = [(warm_codes, warm_plane[:])] * (WARM_UP_PASSES - 1) + [(w1_codes[:], first_picked[:, 0:H])]
+        for moving_codes, moving_plane in warm_moving:
             nc.tensor.matmul_mx(
-                out=warm_bank[:, 0 : PAIR * P],
+                out=warm_bank[:, 0 : moving_plane.shape[1]],
                 lhsT=warm_codes[:, 0:P].bitcast(FP8X4),
                 lhsT_scale=warm_plane[:, 0:P],
-                rhs=warm_codes[:].bitcast(FP8X4),
-                rhs_scale=warm_plane[:],
+                rhs=moving_codes.bitcast(FP8X4),
+                rhs_scale=moving_plane,
                 start=True,
                 stop=True,
             )
@@ -121,7 +138,6 @@ def tile_picked_phmlp_relu_p_kernel(tc, x_words, x_scales, w1, w2_words, w2_scal
 
         def first_layer(c):
             u, in_unit = divmod(c, PER_UNIT)
-            v, in_half = divmod(c, HALF // CHUNK)
             h_bank = psum.tile([P, PACK, CHUNK], F32, name="h_bank", tag="bank")
             for t in range(PACK):
                 pair_codes, pair_plane = w1_pairs[t - t % PAIR]
@@ -131,7 +147,7 @@ def tile_picked_phmlp_relu_p_kernel(tc, x_words, x_scales, w1, w2_words, w2_scal
                     lhsT=pair_codes[:, columns].bitcast(FP8X4),
                     lhsT_scale=pair_plane[:, columns],
                     rhs=xw_picked[u][:, in_unit * CHUNK : (in_unit + 1) * CHUNK].bitcast(FP8X4),
-                    rhs_scale=xs_planes[v][:, in_half * CHUNK : (in_half + 1) * CHUNK],
+                    rhs_scale=xs_plane[:, c * CHUNK : (c + 1) * CHUNK],
                     start=True,
                     stop=True,
                 )

@@ -22,14 +22,15 @@ GROUP = 16
 BLOCK_ROWS = 8
 BANKS = 8
 
-FIRST = 736
+HALF = 512
 UNIT = 256
 CHUNK = 128
-UNITS, CHUNKS = S // UNIT, S // CHUNK
+HALVES, UNITS, CHUNKS = S // HALF, S // UNIT, S // CHUNK
 PER_UNIT = UNIT // CHUNK
 OUT_BLOCKS = N // P
 PAIR = 2
 WARM_UP_PASSES = 4
+GROUPS = ((0, 1), (2, 3), (4, 5), (6,), (7,))
 CAST_SPLIT = 64
 
 VECTOR_RELU = (2, 4)
@@ -42,15 +43,15 @@ def tile_picked_phmlp_relu_p_kernel(tc, x_words, x_scales, w1, w2_words, w2_scal
         psum = ctx.enter_context(tc.psum_pool(name="psum", bufs=BANKS))
 
         load_turn = dict(tag="load_turn", bufs=1 + 2, align_bytes=64)
-        vector_slots = 2 + PACK // PAIR + 1 + UNITS + len(VECTOR_RELU) + UNITS + (UNITS - 1)
+        vector_slots = HALVES + PACK // PAIR + 2 + UNITS + len(VECTOR_RELU) + len(GROUPS) + 4
+        scalar_turn = dict(tag="scalar_turn", bufs=7, align_bytes=64)
         vector_turn = dict(tag="vector_turn", bufs=vector_slots, align_bytes=64)
 
         xs_table = keep.tile([P, T], U8, name="xs_table", align_bytes=64)
         nc.vector.memset(xs_table[:].bitcast(I32), 0)
-        w2_plane = keep.tile([P, N], U8, name="w2_plane", align_bytes=64)
-        nc.vector.memset(w2_plane[:].bitcast(I32), 0)
-        xs_plane = keep.tile([P, S], U8, name="xs_plane", **load_turn)
-        nc.vector.memset(xs_plane[:].bitcast(I32), 0)
+        first_plane = keep.tile([P, HALF], U8, name="xs_plane0", **load_turn)
+        nc.vector.memset(first_plane[:].bitcast(I32), 0)
+        xs_planes = [first_plane, keep.tile([P, HALF], U8, name="xs_plane1", align_bytes=64)]
 
         w1_rows = w1.rearrange("(p j) c -> p j c", j=PACK)
         w1_head = keep.tile([P, 1, H], F32, name="w1_head")
@@ -60,33 +61,25 @@ def tile_picked_phmlp_relu_p_kernel(tc, x_words, x_scales, w1, w2_words, w2_scal
         nc.sync.dma_start(xs_table[0:P:BLOCK_ROWS, :].bitcast(I32), x_scales[0].bitcast(I32))
         w1_rest = keep.tile([P, PACK - 1, H], F32, name="w1_rest", **load_turn)
         nc.sync.dma_start(w1_rest[:], w1_rows[:, 1:PACK, :])
-
-        def load_w2_scales(q):
-            w2_rows = w2_scales[0, PACK * q : PACK * (q + 1), :]
-            nc.sync.dma_start(w2_plane[QUAD * q : QUAD * q + PACK, :].bitcast(I32), w2_rows.bitcast(I32))
-
-        for q in range(P // QUAD - 1):
-            load_w2_scales(q)
         xw_table = keep.tile([P, T], U32, name="xw_table", **load_turn)
         nc.sync.dma_start(xw_table[:].bitcast(I32), x_words[0].rearrange("p n t -> p (n t)").bitcast(I32))
-        load_w2_scales(P // QUAD - 1)
 
-        def pick_scales(lo, hi):
-            picked = keep.tile([P, hi - lo], U8, name=f"xs_picked{lo}", **vector_turn)
-            nc.vector.tensor_copy(picked[:], xs_table[:].indirect(offsets[:, lo // GROUP : hi // GROUP]))
-            for r in range(PACK):
-                nc.sync.dma_start(xs_plane[r:P:QUAD, lo:hi].bitcast(I32), picked[BLOCK_ROWS * r : P : QUAD, :].bitcast(I32))
-            return picked
-
-        first_picked = pick_scales(0, FIRST)
+        for v in range(HALVES):
+            xs_picked = keep.tile([P, HALF], U8, name=f"xs_picked{v}", **vector_turn)
+            entries = offsets[:, v * (HALF // GROUP) : (v + 1) * (HALF // GROUP)]
+            nc.vector.tensor_copy(xs_picked[:], xs_table[:].indirect(entries))
+            if v > 0:
+                nc.vector.tensor_copy(xs_planes[v][:].bitcast(I32), xs_picked[:].bitcast(I32))
+            for r in range(min(v, 1), PACK):
+                nc.sync.dma_start(xs_planes[v][r:P:QUAD, :].bitcast(I32), xs_picked[BLOCK_ROWS * r : P : QUAD, :].bitcast(I32))
 
         w1_bf = {first_tile: keep.tile([P, PAIR, P, PACK], BF16, name=f"w1_bf{first_tile}", align_bytes=64) for first_tile in (PAIR, 0)}
         head_src = w1_head[:, 0, :].rearrange("p (n e t) -> p n t e", e=2, t=PACK)
         rest_src = w1_rest[:].rearrange("p j (m t) -> p m t j", t=PACK)
         shares = (
-            (nc.vector.tensor_copy, PAIR, 0, CAST_SPLIT),
-            (nc.scalar.copy, PAIR, CAST_SPLIT, P),
-            (nc.scalar.copy, 0, 0, P),
+            (nc.scalar.copy, PAIR, 0, P),
+            (nc.vector.tensor_copy, 0, 0, CAST_SPLIT),
+            (nc.scalar.copy, 0, CAST_SPLIT, P),
         )
         for cast, first_tile, lo, hi in shares:
             head_dst = w1_bf[first_tile][:, :, :, 0].rearrange("p t (n e) -> p n t e", e=2)
@@ -96,32 +89,30 @@ def tile_picked_phmlp_relu_p_kernel(tc, x_words, x_scales, w1, w2_words, w2_scal
             cast(rest_dst[:, lo:hi, :, 1:PACK], rest_src[:, lo:hi, first_tile : first_tile + PAIR])
 
         w1_pairs = {}
-        w1_codes = keep.tile([P, PACK * P], U32, name="w1_codes", align_bytes=64)
-
-        def quantise_pair(first_tile):
-            pair_codes = w1_codes[:, first_tile * P : (first_tile + PAIR) * P]
-            pair_plane = keep.tile([P, PAIR * P], U8, name=f"w1_plane{first_tile}", **vector_turn)
+        for first_tile in (PAIR, 0):
+            pair_codes = keep.tile([P, PAIR * P], U32, name=f"w1_codes{first_tile}", **vector_turn)
+            pair_plane = keep.tile([P, PAIR * P], U8, name=f"w1_plane{first_tile}", align_bytes=64)
             pair_bf = w1_bf[first_tile][:].rearrange("p t m j -> p (t m j)")
-            nc.vector.quantize_mx(out=pair_codes.bitcast(FP8X4), scales=pair_plane[:], in_=pair_bf)
+            nc.vector.quantize_mx(out=pair_codes[:].bitcast(FP8X4), scales=pair_plane[:], in_=pair_bf)
             w1_pairs[first_tile] = (pair_codes, pair_plane)
-
-        quantise_pair(PAIR)
-        pick_scales(FIRST, S)
-        quantise_pair(0)
 
         w2_codes = keep.tile([P, 2 * N], U8, name="w2_codes", **vector_turn)
         nc.sync.dma_start(w2_codes[:].bitcast(I32), w2_words[0].bitcast(I32))
+        w2_plane = keep.tile([P, N], U8, name="w2_plane", **vector_turn)
+        nc.vector.memset(w2_plane[:].bitcast(I32), 0)
+        for q in range(P // QUAD):
+            w2_rows = w2_scales[0, PACK * q : PACK * (q + 1), :]
+            nc.sync.dma_start(w2_plane[QUAD * q : QUAD * q + PACK, :].bitcast(I32), w2_rows.bitcast(I32))
 
         warm_codes, warm_plane = w1_pairs[PAIR]
         warm_bank = psum.tile([P, H], F32, name="warm_bank", tag="bank")
-        warm_moving = [(warm_codes, warm_plane[:])] * (WARM_UP_PASSES - 1) + [(w1_codes[:], first_picked[:, 0:H])]
-        for moving_codes, moving_plane in warm_moving:
+        for warm_pass in range(WARM_UP_PASSES):
             nc.tensor.matmul_mx(
-                out=warm_bank[:, 0 : moving_plane.shape[1]],
+                out=warm_bank[:, 0 : PAIR * P],
                 lhsT=warm_codes[:, 0:P].bitcast(FP8X4),
                 lhsT_scale=warm_plane[:, 0:P],
-                rhs=moving_codes.bitcast(FP8X4),
-                rhs_scale=moving_plane,
+                rhs=warm_codes[:].bitcast(FP8X4),
+                rhs_scale=warm_plane[:],
                 start=True,
                 stop=True,
             )
@@ -138,6 +129,7 @@ def tile_picked_phmlp_relu_p_kernel(tc, x_words, x_scales, w1, w2_words, w2_scal
 
         def first_layer(c):
             u, in_unit = divmod(c, PER_UNIT)
+            v, in_half = divmod(c, HALF // CHUNK)
             h_bank = psum.tile([P, PACK, CHUNK], F32, name="h_bank", tag="bank")
             for t in range(PACK):
                 pair_codes, pair_plane = w1_pairs[t - t % PAIR]
@@ -147,32 +139,38 @@ def tile_picked_phmlp_relu_p_kernel(tc, x_words, x_scales, w1, w2_words, w2_scal
                     lhsT=pair_codes[:, columns].bitcast(FP8X4),
                     lhsT_scale=pair_plane[:, columns],
                     rhs=xw_picked[u][:, in_unit * CHUNK : (in_unit + 1) * CHUNK].bitcast(FP8X4),
-                    rhs_scale=xs_plane[:, c * CHUNK : (c + 1) * CHUNK],
+                    rhs_scale=xs_planes[v][:, in_half * CHUNK : (in_half + 1) * CHUNK],
                     start=True,
                     stop=True,
                 )
             h_banks[c] = h_bank
 
-        def relu(c):
-            u, in_unit = divmod(c, PER_UNIT)
-            if in_unit == 0:
-                placing = vector_turn if c in VECTOR_RELU else dict(align_bytes=64)
-                h_bf[u] = keep.tile([P, UNIT, PACK], BF16, name=f"h_bf{u}", **placing)
-            h_dst = h_bf[u][:, in_unit * CHUNK : (in_unit + 1) * CHUNK, :]
+        def relu(g, c):
+            in_group = c - GROUPS[g][0]
+            if in_group == 0:
+                placing = vector_turn if c in VECTOR_RELU else scalar_turn
+                h_bf[g] = keep.tile([P, len(GROUPS[g]) * CHUNK, PACK], BF16, name=f"h_bf{g}", **placing)
+            h_dst = h_bf[g][:, in_group * CHUNK : (in_group + 1) * CHUNK, :]
             h_src = h_banks[c][:].rearrange("p t n -> p n t")
             if c in VECTOR_RELU:
                 nc.vector.tensor_scalar_max(h_dst, h_src, 0.0)
             else:
                 nc.scalar.activation(h_dst, h_src, RELU)
 
-        def second_layer(u, bank_each):
-            h_codes = keep.tile([P, UNIT], U32, name=f"h_codes{u}", **vector_turn)
-            h_plane = keep.tile([P, UNIT], U8, name=f"h_plane{u}", align_bytes=64)
-            nc.vector.quantize_mx(out=h_codes[:].bitcast(FP8X4), scales=h_plane[:], in_=h_bf[u][:].rearrange("p n t -> p (n t)"))
-
-            def product(dst, a):
+        def second_layer(g, bank_each):
+            width = len(GROUPS[g]) * CHUNK
+            h_codes = keep.tile([P, width], U32, name=f"h_codes{g}", **vector_turn)
+            h_plane = keep.tile([P, width], U8, name=f"h_plane{g}", align_bytes=64)
+            nc.vector.quantize_mx(out=h_codes[:].bitcast(FP8X4), scales=h_plane[:], in_=h_bf[g][:].rearrange("p n t -> p (n t)"))
+            if bank_each:
+                banks = [psum.tile([P, 1, width], F32, name="block_bank", tag="bank") for a in range(OUT_BLOCKS)]
+                out_banks[g] = [banks[a][:, 0:1, :] for a in range(OUT_BLOCKS)]
+            else:
+                bank = psum.tile([P, OUT_BLOCKS, width], F32, name="out_bank", tag="bank")
+                out_banks[g] = [bank[:, a : a + 1, :] for a in range(OUT_BLOCKS)] + [bank[:]]
+            for a in range(OUT_BLOCKS):
                 nc.tensor.matmul_mx(
-                    out=dst,
+                    out=out_banks[g][a][:, 0, :],
                     lhsT=w2_codes[:, a * 2 * P : (a + 1) * 2 * P].bitcast(FP4X4),
                     lhsT_scale=w2_plane[:, a * P : (a + 1) * P],
                     rhs=h_codes[:].bitcast(FP8X4),
@@ -181,41 +179,40 @@ def tile_picked_phmlp_relu_p_kernel(tc, x_words, x_scales, w1, w2_words, w2_scal
                     stop=True,
                 )
 
-            if bank_each:
-                out_banks[u] = []
-                for a in range(OUT_BLOCKS):
-                    block_bank = psum.tile([P, UNIT], F32, name="block_bank", tag="bank")
-                    product(block_bank[:], a)
-                    out_banks[u].append(block_bank)
-            else:
-                out_bank = psum.tile([P, OUT_BLOCKS, UNIT], F32, name="out_bank", tag="bank")
-                for a in range(OUT_BLOCKS):
-                    product(out_bank[:, a, :], a)
-                out_banks[u] = out_bank
+        def places(g):
+            return slice(GROUPS[g][0] * CHUNK, (GROUPS[g][-1] + 1) * CHUNK)
 
-        def store(u, result):
-            nc.sync.dma_start(out_rows[:, :, u * UNIT : (u + 1) * UNIT], result[:])
+        def leave(g, a, on_vector):
+            source = out_banks[g][a]
+            result = keep.tile(source.shape, F32, name=f"result{g}_{a}", **(vector_turn if on_vector else scalar_turn))
+            if on_vector:
+                nc.vector.tensor_copy(result[:], source)
+            else:
+                nc.scalar.copy(result[:], source)
+            rows = out_rows if a == OUT_BLOCKS else out_rows[:, a : a + 1]
+            nc.sync.dma_start(rows[:, :, places(g)], result[:])
 
         for c in range(CHUNKS):
             first_layer(c)
-            if c < 2 * PER_UNIT:
-                relu(c)
+        for g in range(2):
+            for c in GROUPS[g]:
+                relu(g, c)
         second_layer(0, bank_each=False)
-        for c in range(2 * PER_UNIT, CHUNKS):
-            relu(c)
+        for g in range(2, 4):
+            for c in GROUPS[g]:
+                relu(g, c)
         second_layer(1, bank_each=False)
-
-        result0 = keep.tile([P, OUT_BLOCKS, UNIT], F32, name="result0", **vector_turn)
-        nc.vector.tensor_copy(result0[:], out_banks[0][:])
-        store(0, result0)
-        for u in range(2, UNITS):
-            second_layer(u, bank_each=True)
-
-        result1 = keep.tile([P, OUT_BLOCKS, UNIT], F32, name="result1")
-        nc.scalar.copy(result1[:], out_banks[1][:])
-        store(1, result1)
-        for u in range(2, UNITS):
-            result = keep.tile([P, OUT_BLOCKS, UNIT], F32, name=f"result{u}", **vector_turn)
-            nc.vector.tensor_copy(result[:, 1, :], out_banks[u][1][:])
-            nc.scalar.copy(result[:, 0, :], out_banks[u][0][:])
-            store(u, result)
+        second_layer(2, bank_each=False)
+        second_layer(3, bank_each=False)
+        for a in range(OUT_BLOCKS):
+            leave(0, a, on_vector=False)
+        relu(4, 7)
+        for a in range(OUT_BLOCKS):
+            leave(1, a, on_vector=True)
+        second_layer(4, bank_each=True)
+        leave(2, OUT_BLOCKS, on_vector=False)
+        leave(3, OUT_BLOCKS, on_vector=True)
+        last = keep.tile([P, OUT_BLOCKS, CHUNK], F32, name="last", **vector_turn)
+        nc.vector.tensor_copy(last[:, 0:1, :], out_banks[4][0])
+        nc.scalar.copy(last[:, 1:2, :], out_banks[4][1])
+        nc.sync.dma_start(out_rows[:, :, places(4)], last[:])

@@ -44,7 +44,7 @@ def tile_picked_phmlp_relu_p_kernel(tc, x_words, x_scales, w1, w2_words, w2_scal
 
         load_turn = dict(tag="load_turn", bufs=1 + 2, align_bytes=64)
         vector_slots = HALVES + PACK // PAIR + 2 + UNITS + len(VECTOR_RELU) + len(GROUPS) + 4
-        scalar_turn = dict(tag="scalar_turn", bufs=7, align_bytes=64)
+        scalar_turn = dict(tag="scalar_turn", bufs=8, align_bytes=64)
         vector_turn = dict(tag="vector_turn", bufs=vector_slots, align_bytes=64)
 
         xs_table = keep.tile([P, T], U8, name="xs_table", align_bytes=64)
@@ -197,21 +197,20 @@ def tile_picked_phmlp_relu_p_kernel(tc, x_words, x_scales, w1, w2_words, w2_scal
         for g in range(2):
             for c in GROUPS[g]:
                 relu(g, c)
-        second_layer(0, bank_each=False)
+        second_layer(0, bank_each=True)
         for g in range(2, 4):
             for c in GROUPS[g]:
                 relu(g, c)
-        second_layer(1, bank_each=False)
-        second_layer(2, bank_each=False)
-        second_layer(3, bank_each=False)
-        for a in range(OUT_BLOCKS):
-            leave(0, a, on_vector=False)
+        for g in range(1, 4):
+            second_layer(g, bank_each=False)
+        leave(0, 0, on_vector=False)
+        leave(0, 1, on_vector=True)
         relu(4, 7)
         for a in range(OUT_BLOCKS):
             leave(1, a, on_vector=True)
         second_layer(4, bank_each=True)
         leave(2, OUT_BLOCKS, on_vector=False)
-        leave(3, OUT_BLOCKS, on_vector=True)
+        leave(3, OUT_BLOCKS, on_vector=False)
         last = keep.tile([P, OUT_BLOCKS, CHUNK], F32, name="last", **vector_turn)
         nc.vector.tensor_copy(last[:, 0:1, :], out_banks[4][0])
         nc.scalar.copy(last[:, 1:2, :], out_banks[4][1])

@@ -64,8 +64,10 @@ def tile_picked_phmlp_relu_p_kernel(tc, x_words, x_scales, w1, w2_words, w2_scal
         xw_table = keep.tile([P, T], U32, name="xw_table", **load_turn)
         nc.sync.dma_start(xw_table[:].bitcast(I32), x_words[0].rearrange("p n t -> p (n t)").bitcast(I32))
 
+        picked_halves = []
         for v in range(HALVES):
             xs_picked = keep.tile([P, HALF], U8, name=f"xs_picked{v}", **vector_turn)
+            picked_halves.append(xs_picked)
             entries = offsets[:, v * (HALF // GROUP) : (v + 1) * (HALF // GROUP)]
             nc.vector.tensor_copy(xs_picked[:], xs_table[:].indirect(entries))
             if v > 0:
@@ -89,11 +91,12 @@ def tile_picked_phmlp_relu_p_kernel(tc, x_words, x_scales, w1, w2_words, w2_scal
             cast(rest_dst[:, lo:hi, :, 1:PACK], rest_src[:, lo:hi, first_tile : first_tile + PAIR])
 
         w1_pairs = {}
+        w1_codes = keep.tile([P, PACK * P], U32, name="w1_codes", align_bytes=64)
         for first_tile in (PAIR, 0):
-            pair_codes = keep.tile([P, PAIR * P], U32, name=f"w1_codes{first_tile}", **vector_turn)
-            pair_plane = keep.tile([P, PAIR * P], U8, name=f"w1_plane{first_tile}", align_bytes=64)
+            pair_codes = w1_codes[:, first_tile * P : (first_tile + PAIR) * P]
+            pair_plane = keep.tile([P, PAIR * P], U8, name=f"w1_plane{first_tile}", **vector_turn)
             pair_bf = w1_bf[first_tile][:].rearrange("p t m j -> p (t m j)")
-            nc.vector.quantize_mx(out=pair_codes[:].bitcast(FP8X4), scales=pair_plane[:], in_=pair_bf)
+            nc.vector.quantize_mx(out=pair_codes.bitcast(FP8X4), scales=pair_plane[:], in_=pair_bf)
             w1_pairs[first_tile] = (pair_codes, pair_plane)
 
         w2_codes = keep.tile([P, 2 * N], U8, name="w2_codes", **vector_turn)
@@ -106,13 +109,14 @@ def tile_picked_phmlp_relu_p_kernel(tc, x_words, x_scales, w1, w2_words, w2_scal
 
         warm_codes, warm_plane = w1_pairs[PAIR]
         warm_bank = psum.tile([P, H], F32, name="warm_bank", tag="bank")
-        for warm_pass in range(WARM_UP_PASSES):
+        warm_moving = [(warm_codes, warm_plane[:])] * (WARM_UP_PASSES - 1) + [(w1_codes[:], picked_halves[0][:])]
+        for moving_codes, moving_plane in warm_moving:
             nc.tensor.matmul_mx(
-                out=warm_bank[:, 0 : PAIR * P],
+                out=warm_bank[:, 0 : moving_plane.shape[1]],
                 lhsT=warm_codes[:, 0:P].bitcast(FP8X4),
                 lhsT_scale=warm_plane[:, 0:P],
-                rhs=warm_codes[:].bitcast(FP8X4),
-                rhs_scale=warm_plane[:],
+                rhs=moving_codes.bitcast(FP8X4),
+                rhs_scale=moving_plane,
                 start=True,
                 stop=True,
             )

@@ -29,7 +29,7 @@ HALVES, UNITS, CHUNKS = S // HALF, S // UNIT, S // CHUNK
 PER_UNIT = UNIT // CHUNK
 OUT_BLOCKS = N // P
 PAIR = 2
-WARM_UP_PASSES = 4
+WARM_UP_PASSES = 2
 GROUPS = ((0, 1), (2, 3), (4, 5), (6,), (7,))
 CAST_SPLIT = 64
 
@@ -42,8 +42,8 @@ def tile_picked_phmlp_relu_p_kernel(tc, x_words, x_scales, w1, w2_words, w2_scal
         keep = ctx.enter_context(tc.tile_pool(name="keep", bufs=1))
         psum = ctx.enter_context(tc.psum_pool(name="psum", bufs=BANKS))
 
-        load_turn = dict(tag="load_turn", bufs=1 + 2, align_bytes=64)
-        vector_slots = HALVES + PACK // PAIR + 2 + UNITS + len(VECTOR_RELU) + len(GROUPS) + 4
+        load_turn = dict(tag="load_turn", bufs=1 + 3, align_bytes=64)
+        vector_slots = HALVES + PACK // PAIR + 1 + UNITS + len(VECTOR_RELU) + len(GROUPS) + 4
         scalar_turn = dict(tag="scalar_turn", bufs=8, align_bytes=64)
         vector_turn = dict(tag="vector_turn", bufs=vector_slots, align_bytes=64)
 
@@ -64,10 +64,11 @@ def tile_picked_phmlp_relu_p_kernel(tc, x_words, x_scales, w1, w2_words, w2_scal
         xw_table = keep.tile([P, T], U32, name="xw_table", **load_turn)
         nc.sync.dma_start(xw_table[:].bitcast(I32), x_words[0].rearrange("p n t -> p (n t)").bitcast(I32))
 
-        picked_halves = []
+        w2_codes = keep.tile([P, 2 * N], U8, name="w2_codes", **load_turn)
+        nc.sync.dma_start(w2_codes[:].bitcast(I32), w2_words[0].bitcast(I32))
+
         for v in range(HALVES):
             xs_picked = keep.tile([P, HALF], U8, name=f"xs_picked{v}", **vector_turn)
-            picked_halves.append(xs_picked)
             entries = offsets[:, v * (HALF // GROUP) : (v + 1) * (HALF // GROUP)]
             nc.vector.tensor_copy(xs_picked[:], xs_table[:].indirect(entries))
             if v > 0:
@@ -99,8 +100,6 @@ def tile_picked_phmlp_relu_p_kernel(tc, x_words, x_scales, w1, w2_words, w2_scal
             nc.vector.quantize_mx(out=pair_codes.bitcast(FP8X4), scales=pair_plane[:], in_=pair_bf)
             w1_pairs[first_tile] = (pair_codes, pair_plane)
 
-        w2_codes = keep.tile([P, 2 * N], U8, name="w2_codes", **vector_turn)
-        nc.sync.dma_start(w2_codes[:].bitcast(I32), w2_words[0].bitcast(I32))
         w2_plane = keep.tile([P, N], U8, name="w2_plane", **vector_turn)
         nc.vector.memset(w2_plane[:].bitcast(I32), 0)
         for q in range(P // QUAD):
@@ -108,15 +107,14 @@ def tile_picked_phmlp_relu_p_kernel(tc, x_words, x_scales, w1, w2_words, w2_scal
             nc.sync.dma_start(w2_plane[QUAD * q : QUAD * q + PACK, :].bitcast(I32), w2_rows.bitcast(I32))
 
         warm_codes, warm_plane = w1_pairs[PAIR]
-        warm_bank = psum.tile([P, H], F32, name="warm_bank", tag="bank")
-        warm_moving = [(warm_codes, warm_plane[:])] * (WARM_UP_PASSES - 1) + [(w1_codes[:], picked_halves[0][:])]
-        for moving_codes, moving_plane in warm_moving:
+        warm_bank = psum.tile([P, WARM_UP_PASSES, N], F32, name="warm_bank", tag="bank")
+        for n in range(WARM_UP_PASSES):
             nc.tensor.matmul_mx(
-                out=warm_bank[:, 0 : moving_plane.shape[1]],
+                out=warm_bank[:, n, :],
                 lhsT=warm_codes[:, 0:P].bitcast(FP8X4),
                 lhsT_scale=warm_plane[:, 0:P],
-                rhs=moving_codes.bitcast(FP8X4),
-                rhs_scale=moving_plane,
+                rhs=w2_codes[:].bitcast(FP4X4),
+                rhs_scale=warm_plane[:],
                 start=True,
                 stop=True,
             )
@@ -196,6 +194,12 @@ def tile_picked_phmlp_relu_p_kernel(tc, x_words, x_scales, w1, w2_words, w2_scal
             rows = out_rows if a == OUT_BLOCKS else out_rows[:, a : a + 1]
             nc.sync.dma_start(rows[:, :, places(g)], result[:])
 
+        def leave_shared(g, placing):
+            result = keep.tile([P, OUT_BLOCKS, len(GROUPS[g]) * CHUNK], F32, name=f"result{g}", **placing)
+            nc.scalar.copy(result[:, 0:1, :], out_banks[g][0])
+            nc.vector.tensor_copy(result[:, 1:2, :], out_banks[g][1])
+            nc.sync.dma_start(out_rows[:, :, places(g)], result[:])
+
         for c in range(CHUNKS):
             first_layer(c)
         for g in range(2):
@@ -205,17 +209,15 @@ def tile_picked_phmlp_relu_p_kernel(tc, x_words, x_scales, w1, w2_words, w2_scal
         for g in range(2, 4):
             for c in GROUPS[g]:
                 relu(g, c)
-        for g in range(1, 4):
-            second_layer(g, bank_each=False)
-        leave(0, 0, on_vector=False)
-        leave(0, 1, on_vector=True)
+        second_layer(1, bank_each=True)
+        leave(0, 0, on_vector=True)
+        second_layer(2, bank_each=True)
+        leave(0, 1, on_vector=False)
+        second_layer(3, bank_each=False)
         relu(4, 7)
-        for a in range(OUT_BLOCKS):
-            leave(1, a, on_vector=True)
+        leave(1, 0, on_vector=True)
+        leave(1, 1, on_vector=False)
         second_layer(4, bank_each=True)
-        leave(2, OUT_BLOCKS, on_vector=False)
+        leave_shared(2, scalar_turn)
         leave(3, OUT_BLOCKS, on_vector=False)
-        last = keep.tile([P, OUT_BLOCKS, CHUNK], F32, name="last", **vector_turn)
-        nc.vector.tensor_copy(last[:, 0:1, :], out_banks[4][0])
-        nc.scalar.copy(last[:, 1:2, :], out_banks[4][1])
-        nc.sync.dma_start(out_rows[:, :, places(4)], last[:])
+        leave_shared(4, vector_turn)

@@ -30,6 +30,7 @@ PER_UNIT = UNIT // CHUNK
 OUT_BLOCKS = N // P
 PAIR = 2
 WARM_UP_PASSES = 2
+WARM_UP_LEAD = 64
 GROUPS = ((0, 1), (2, 3), (4, 5), (6,), (7,))
 CAST_SPLIT = 64
 
@@ -107,14 +108,16 @@ def tile_picked_phmlp_relu_p_kernel(tc, x_words, x_scales, w1, w2_words, w2_scal
             nc.sync.dma_start(w2_plane[QUAD * q : QUAD * q + PACK, :].bitcast(I32), w2_rows.bitcast(I32))
 
         warm_codes, warm_plane = w1_pairs[PAIR]
-        warm_bank = psum.tile([P, WARM_UP_PASSES, N], F32, name="warm_bank", tag="bank")
-        for n in range(WARM_UP_PASSES):
+        warm_bank = psum.tile([P, N], F32, name="warm_bank", tag="bank")
+        warm_moving = [warm_codes[:, 0:WARM_UP_LEAD].bitcast(FP8X4)] + [w2_codes[:].bitcast(FP4X4)] * WARM_UP_PASSES
+        for moving in warm_moving:
+            width = moving.shape[1]
             nc.tensor.matmul_mx(
-                out=warm_bank[:, n, :],
+                out=warm_bank[:, 0:width],
                 lhsT=warm_codes[:, 0:P].bitcast(FP8X4),
                 lhsT_scale=warm_plane[:, 0:P],
-                rhs=w2_codes[:].bitcast(FP4X4),
-                rhs_scale=warm_plane[:],
+                rhs=moving,
+                rhs_scale=warm_plane[:, 0:width],
                 start=True,
                 stop=True,
             )
@@ -127,7 +130,7 @@ def tile_picked_phmlp_relu_p_kernel(tc, x_words, x_scales, w1, w2_words, w2_scal
             xw_picked.append(words)
 
         out_rows = out.rearrange("(a p) s -> p a s", p=P)
-        h_banks, h_bf, out_banks = {}, {}, {}
+        h_banks, h_bf, h_codes, h_planes, out_banks = {}, {}, {}, {}, {}
 
         def first_layer(c):
             u, in_unit = divmod(c, PER_UNIT)
@@ -159,11 +162,17 @@ def tile_picked_phmlp_relu_p_kernel(tc, x_words, x_scales, w1, w2_words, w2_scal
             else:
                 nc.scalar.activation(h_dst, h_src, RELU)
 
+        def quantise(g, chunks):
+            width = len(GROUPS[g]) * CHUNK
+            if chunks[0] == GROUPS[g][0]:
+                h_codes[g] = keep.tile([P, width], U32, name=f"h_codes{g}", **vector_turn)
+                h_planes[g] = keep.tile([P, width], U8, name=f"h_plane{g}", align_bytes=64)
+            columns = slice((chunks[0] - GROUPS[g][0]) * CHUNK, (chunks[-1] + 1 - GROUPS[g][0]) * CHUNK)
+            h_in = h_bf[g][:, columns, :].rearrange("p n t -> p (n t)")
+            nc.vector.quantize_mx(out=h_codes[g][:, columns].bitcast(FP8X4), scales=h_planes[g][:, columns], in_=h_in)
+
         def second_layer(g, bank_each):
             width = len(GROUPS[g]) * CHUNK
-            h_codes = keep.tile([P, width], U32, name=f"h_codes{g}", **vector_turn)
-            h_plane = keep.tile([P, width], U8, name=f"h_plane{g}", align_bytes=64)
-            nc.vector.quantize_mx(out=h_codes[:].bitcast(FP8X4), scales=h_plane[:], in_=h_bf[g][:].rearrange("p n t -> p (n t)"))
             if bank_each:
                 banks = [psum.tile([P, 1, width], F32, name="block_bank", tag="bank") for a in range(OUT_BLOCKS)]
                 out_banks[g] = [banks[a][:, 0:1, :] for a in range(OUT_BLOCKS)]
@@ -175,49 +184,47 @@ def tile_picked_phmlp_relu_p_kernel(tc, x_words, x_scales, w1, w2_words, w2_scal
                     out=out_banks[g][a][:, 0, :],
                     lhsT=w2_codes[:, a * 2 * P : (a + 1) * 2 * P].bitcast(FP4X4),
                     lhsT_scale=w2_plane[:, a * P : (a + 1) * P],
-                    rhs=h_codes[:].bitcast(FP8X4),
-                    rhs_scale=h_plane[:],
+                    rhs=h_codes[g][:].bitcast(FP8X4),
+                    rhs_scale=h_planes[g][:],
                     start=True,
                     stop=True,
                 )
 
-        def places(g):
-            return slice(GROUPS[g][0] * CHUNK, (GROUPS[g][-1] + 1) * CHUNK)
-
         def leave(g, a, on_vector):
-            source = out_banks[g][a]
-            result = keep.tile(source.shape, F32, name=f"result{g}_{a}", **(vector_turn if on_vector else scalar_turn))
+            result = keep.tile([P, 1, UNIT], F32, name=f"result{g}_{a}", **(vector_turn if on_vector else scalar_turn))
             if on_vector:
-                nc.vector.tensor_copy(result[:], source)
+                nc.vector.tensor_copy(result[:], out_banks[g][a])
             else:
-                nc.scalar.copy(result[:], source)
-            rows = out_rows if a == OUT_BLOCKS else out_rows[:, a : a + 1]
-            nc.sync.dma_start(rows[:, :, places(g)], result[:])
+                nc.scalar.copy(result[:], out_banks[g][a])
+            nc.sync.dma_start(out_rows[:, a : a + 1, g * UNIT : (g + 1) * UNIT], result[:])
 
-        def leave_shared(g, placing):
-            result = keep.tile([P, OUT_BLOCKS, len(GROUPS[g]) * CHUNK], F32, name=f"result{g}", **placing)
-            nc.scalar.copy(result[:, 0:1, :], out_banks[g][0])
-            nc.vector.tensor_copy(result[:, 1:2, :], out_banks[g][1])
-            nc.sync.dma_start(out_rows[:, :, places(g)], result[:])
-
-        for c in range(CHUNKS):
+        for c in range(CHUNKS - 1):
             first_layer(c)
-        for g in range(2):
-            for c in GROUPS[g]:
-                relu(g, c)
+        relu(0, 0)
+        quantise(0, (0,))
+        relu(0, 1)
+        relu(1, 2)
+        quantise(0, (1,))
         second_layer(0, bank_each=True)
-        for g in range(2, 4):
+        first_layer(CHUNKS - 1)
+        relu(1, 3)
+        for g in range(2, 5):
             for c in GROUPS[g]:
                 relu(g, c)
+        quantise(1, GROUPS[1])
         second_layer(1, bank_each=True)
         leave(0, 0, on_vector=True)
+        quantise(2, GROUPS[2])
         second_layer(2, bank_each=True)
-        leave(0, 1, on_vector=False)
-        second_layer(3, bank_each=False)
-        relu(4, 7)
+        leave(0, 1, on_vector=True)
         leave(1, 0, on_vector=True)
         leave(1, 1, on_vector=False)
-        second_layer(4, bank_each=True)
-        leave_shared(2, scalar_turn)
-        leave(3, OUT_BLOCKS, on_vector=False)
-        leave_shared(4, vector_turn)
+        for g in (3, 4):
+            quantise(g, GROUPS[g])
+            second_layer(g, bank_each=False)
+        leave(2, 0, on_vector=False)
+        leave(2, 1, on_vector=True)
+        last = keep.tile([P, OUT_BLOCKS, UNIT], F32, name="last", **scalar_turn)
+        nc.scalar.copy(last[:, :, 0:CHUNK], out_banks[3][OUT_BLOCKS])
+        nc.vector.tensor_copy(last[:, :, CHUNK:UNIT], out_banks[4][OUT_BLOCKS])
+        nc.sync.dma_start(out_rows[:, :, S - UNIT : S], last[:])

@@ -29,8 +29,7 @@ HALVES, UNITS, CHUNKS = S // HALF, S // UNIT, S // CHUNK
 PER_UNIT = UNIT // CHUNK
 OUT_BLOCKS = N // P
 PAIR = 2
-WARM_UP_PASSES = 2
-WARM_UP_LEAD = 64
+WARM_UP_WIDTHS = (512, 64)
 GROUPS = ((0, 1), (2, 3), (4, 5), (6,), (7,))
 CAST_SPLIT = 64
 
@@ -43,7 +42,7 @@ def tile_picked_phmlp_relu_p_kernel(tc, x_words, x_scales, w1, w2_words, w2_scal
         keep = ctx.enter_context(tc.tile_pool(name="keep", bufs=1))
         psum = ctx.enter_context(tc.psum_pool(name="psum", bufs=BANKS))
 
-        load_turn = dict(tag="load_turn", bufs=1 + 3, align_bytes=64)
+        load_turn = dict(tag="load_turn", bufs=1 + 2, align_bytes=64)
         vector_slots = HALVES + PACK // PAIR + 1 + UNITS + len(VECTOR_RELU) + len(GROUPS) + 4
         scalar_turn = dict(tag="scalar_turn", bufs=8, align_bytes=64)
         vector_turn = dict(tag="vector_turn", bufs=vector_slots, align_bytes=64)
@@ -64,9 +63,6 @@ def tile_picked_phmlp_relu_p_kernel(tc, x_words, x_scales, w1, w2_words, w2_scal
         nc.sync.dma_start(w1_rest[:], w1_rows[:, 1:PACK, :])
         xw_table = keep.tile([P, T], U32, name="xw_table", **load_turn)
         nc.sync.dma_start(xw_table[:].bitcast(I32), x_words[0].rearrange("p n t -> p (n t)").bitcast(I32))
-
-        w2_codes = keep.tile([P, 2 * N], U8, name="w2_codes", **load_turn)
-        nc.sync.dma_start(w2_codes[:].bitcast(I32), w2_words[0].bitcast(I32))
 
         for v in range(HALVES):
             xs_picked = keep.tile([P, HALF], U8, name=f"xs_picked{v}", **vector_turn)
@@ -94,30 +90,30 @@ def tile_picked_phmlp_relu_p_kernel(tc, x_words, x_scales, w1, w2_words, w2_scal
 
         w1_pairs = {}
         w1_codes = keep.tile([P, PACK * P], U32, name="w1_codes", align_bytes=64)
+        w1_plane = keep.tile([P, PACK * P], U8, name="w1_plane", **vector_turn)
         for first_tile in (PAIR, 0):
             pair_codes = w1_codes[:, first_tile * P : (first_tile + PAIR) * P]
-            pair_plane = keep.tile([P, PAIR * P], U8, name=f"w1_plane{first_tile}", **vector_turn)
+            pair_plane = w1_plane[:, first_tile * P : (first_tile + PAIR) * P]
             pair_bf = w1_bf[first_tile][:].rearrange("p t m j -> p (t m j)")
-            nc.vector.quantize_mx(out=pair_codes.bitcast(FP8X4), scales=pair_plane[:], in_=pair_bf)
+            nc.vector.quantize_mx(out=pair_codes.bitcast(FP8X4), scales=pair_plane, in_=pair_bf)
             w1_pairs[first_tile] = (pair_codes, pair_plane)
 
+        w2_codes = keep.tile([P, 2 * N], U8, name="w2_codes", **vector_turn)
+        nc.sync.dma_start(w2_codes[:].bitcast(I32), w2_words[0].bitcast(I32))
         w2_plane = keep.tile([P, N], U8, name="w2_plane", **vector_turn)
         nc.vector.memset(w2_plane[:].bitcast(I32), 0)
         for q in range(P // QUAD):
             w2_rows = w2_scales[0, PACK * q : PACK * (q + 1), :]
             nc.sync.dma_start(w2_plane[QUAD * q : QUAD * q + PACK, :].bitcast(I32), w2_rows.bitcast(I32))
 
-        warm_codes, warm_plane = w1_pairs[PAIR]
-        warm_bank = psum.tile([P, N], F32, name="warm_bank", tag="bank")
-        warm_moving = [warm_codes[:, 0:WARM_UP_LEAD].bitcast(FP8X4)] + [w2_codes[:].bitcast(FP4X4)] * WARM_UP_PASSES
-        for moving in warm_moving:
-            width = moving.shape[1]
+        warm_bank = psum.tile([P, H], F32, name="warm_bank", tag="bank")
+        for width in WARM_UP_WIDTHS:
             nc.tensor.matmul_mx(
                 out=warm_bank[:, 0:width],
-                lhsT=warm_codes[:, 0:P].bitcast(FP8X4),
-                lhsT_scale=warm_plane[:, 0:P],
-                rhs=moving,
-                rhs_scale=warm_plane[:, 0:width],
+                lhsT=w1_codes[:, 0:P].bitcast(FP8X4),
+                lhsT_scale=w1_plane[:, 0:P],
+                rhs=w1_codes[:, 0:width].bitcast(FP8X4),
+                rhs_scale=w1_plane[:, 0:width],
                 start=True,
                 stop=True,
             )
@@ -221,10 +217,11 @@ def tile_picked_phmlp_relu_p_kernel(tc, x_words, x_scales, w1, w2_words, w2_scal
         leave(1, 1, on_vector=False)
         for g in (3, 4):
             quantise(g, GROUPS[g])
-            second_layer(g, bank_each=False)
+            second_layer(g, bank_each=True)
         leave(2, 0, on_vector=False)
         leave(2, 1, on_vector=True)
         last = keep.tile([P, OUT_BLOCKS, UNIT], F32, name="last", **scalar_turn)
-        nc.scalar.copy(last[:, :, 0:CHUNK], out_banks[3][OUT_BLOCKS])
-        nc.vector.tensor_copy(last[:, :, CHUNK:UNIT], out_banks[4][OUT_BLOCKS])
+        for n, g in enumerate((3, 4)):
+            nc.scalar.copy(last[:, 0:1, n * CHUNK : (n + 1) * CHUNK], out_banks[g][0])
+            nc.vector.tensor_copy(last[:, 1:2, n * CHUNK : (n + 1) * CHUNK], out_banks[g][1])
         nc.sync.dma_start(out_rows[:, :, S - UNIT : S], last[:])

@@ -31,7 +31,7 @@ OUT_BLOCKS = N // P
 PAIR = 2
 WARM_UP_WIDTHS = (512, 64)
 GROUPS = ((0, 1), (2, 3), (4, 5), (6,), (7,))
-CAST_SPLIT = 64
+CAST_SPLIT = 96
 
 VECTOR_RELU = (2, 4)
 

@@ -30,10 +30,7 @@ PER_UNIT = UNIT // CHUNK
 OUT_BLOCKS = N // P
 PAIR = 2
 WARM_UP_WIDTHS = (512, 64)
-GROUPS = ((0, 1), (2, 3), (4, 5), (6,), (7,))
 CAST_SPLIT = 96
-
-VECTOR_RELU = (2, 4)
 
 
 def tile_picked_phmlp_relu_p_kernel(tc, x_words, x_scales, w1, w2_words, w2_scales, offs, out):
@@ -43,8 +40,8 @@ def tile_picked_phmlp_relu_p_kernel(tc, x_words, x_scales, w1, w2_words, w2_scal
         psum = ctx.enter_context(tc.psum_pool(name="psum", bufs=BANKS))
 
         load_turn = dict(tag="load_turn", bufs=1 + 2, align_bytes=64)
-        vector_slots = HALVES + PACK // PAIR + 1 + UNITS + len(VECTOR_RELU) + len(GROUPS) + 4
-        scalar_turn = dict(tag="scalar_turn", bufs=8, align_bytes=64)
+        vector_slots = 26
+        scalar_turn = dict(tag="scalar_turn", bufs=11, align_bytes=64)
         vector_turn = dict(tag="vector_turn", bufs=vector_slots, align_bytes=64)
 
         xs_table = keep.tile([P, T], U8, name="xs_table", align_bytes=64)
@@ -88,7 +85,6 @@ def tile_picked_phmlp_relu_p_kernel(tc, x_words, x_scales, w1, w2_words, w2_scal
             rest_dst = w1_bf[first_tile][:].rearrange("p t m j -> p m t j")
             cast(rest_dst[:, lo:hi, :, 1:PACK], rest_src[:, lo:hi, first_tile : first_tile + PAIR])
 
-        w1_pairs = {}
         w1_codes = keep.tile([P, PACK * P], U32, name="w1_codes", align_bytes=64)
         w1_plane = keep.tile([P, PACK * P], U8, name="w1_plane", **vector_turn)
         for first_tile in (PAIR, 0):
@@ -96,7 +92,6 @@ def tile_picked_phmlp_relu_p_kernel(tc, x_words, x_scales, w1, w2_words, w2_scal
             pair_plane = w1_plane[:, first_tile * P : (first_tile + PAIR) * P]
             pair_bf = w1_bf[first_tile][:].rearrange("p t m j -> p (t m j)")
             nc.vector.quantize_mx(out=pair_codes.bitcast(FP8X4), scales=pair_plane, in_=pair_bf)
-            w1_pairs[first_tile] = (pair_codes, pair_plane)
 
         w2_codes = keep.tile([P, 2 * N], U8, name="w2_codes", **vector_turn)
         nc.sync.dma_start(w2_codes[:].bitcast(I32), w2_words[0].bitcast(I32))
@@ -131,97 +126,90 @@ def tile_picked_phmlp_relu_p_kernel(tc, x_words, x_scales, w1, w2_words, w2_scal
         def first_layer(c):
             u, in_unit = divmod(c, PER_UNIT)
             v, in_half = divmod(c, HALF // CHUNK)
-            h_bank = psum.tile([P, PACK, CHUNK], F32, name="h_bank", tag="bank")
+            h_banks[c] = psum.tile([P, PACK, CHUNK], F32, name="h_bank", tag="bank")
             for t in range(PACK):
-                pair_codes, pair_plane = w1_pairs[t - t % PAIR]
-                columns = slice(t % PAIR * P, (t % PAIR + 1) * P)
                 nc.tensor.matmul_mx(
-                    out=h_bank[:, t, :],
-                    lhsT=pair_codes[:, columns].bitcast(FP8X4),
-                    lhsT_scale=pair_plane[:, columns],
+                    out=h_banks[c][:, t, :],
+                    lhsT=w1_codes[:, t * P : (t + 1) * P].bitcast(FP8X4),
+                    lhsT_scale=w1_plane[:, t * P : (t + 1) * P],
                     rhs=xw_picked[u][:, in_unit * CHUNK : (in_unit + 1) * CHUNK].bitcast(FP8X4),
                     rhs_scale=xs_planes[v][:, in_half * CHUNK : (in_half + 1) * CHUNK],
                     start=True,
                     stop=True,
                 )
-            h_banks[c] = h_bank
 
-        def relu(g, c):
-            in_group = c - GROUPS[g][0]
-            if in_group == 0:
-                placing = vector_turn if c in VECTOR_RELU else scalar_turn
-                h_bf[g] = keep.tile([P, len(GROUPS[g]) * CHUNK, PACK], BF16, name=f"h_bf{g}", **placing)
-            h_dst = h_bf[g][:, in_group * CHUNK : (in_group + 1) * CHUNK, :]
+        def relu(c, on_vector):
+            h_bf[c] = keep.tile([P, CHUNK, PACK], BF16, name=f"h_bf{c}", **(vector_turn if on_vector else scalar_turn))
             h_src = h_banks[c][:].rearrange("p t n -> p n t")
-            if c in VECTOR_RELU:
-                nc.vector.tensor_scalar_max(h_dst, h_src, 0.0)
+            if on_vector:
+                nc.vector.tensor_scalar_max(h_bf[c][:], h_src, 0.0)
             else:
-                nc.scalar.activation(h_dst, h_src, RELU)
+                nc.scalar.activation(h_bf[c][:], h_src, RELU)
 
-        def quantise(g, chunks):
-            width = len(GROUPS[g]) * CHUNK
-            if chunks[0] == GROUPS[g][0]:
-                h_codes[g] = keep.tile([P, width], U32, name=f"h_codes{g}", **vector_turn)
-                h_planes[g] = keep.tile([P, width], U8, name=f"h_plane{g}", align_bytes=64)
-            columns = slice((chunks[0] - GROUPS[g][0]) * CHUNK, (chunks[-1] + 1 - GROUPS[g][0]) * CHUNK)
-            h_in = h_bf[g][:, columns, :].rearrange("p n t -> p (n t)")
-            nc.vector.quantize_mx(out=h_codes[g][:, columns].bitcast(FP8X4), scales=h_planes[g][:, columns], in_=h_in)
+        def quantise(c):
+            h_codes[c] = keep.tile([P, CHUNK], U32, name=f"h_codes{c}", **vector_turn)
+            h_planes[c] = keep.tile([P, CHUNK], U8, name=f"h_plane{c}", align_bytes=64)
+            nc.vector.quantize_mx(out=h_codes[c][:].bitcast(FP8X4), scales=h_planes[c][:], in_=h_bf[c][:].rearrange("p n t -> p (n t)"))
 
-        def second_layer(g, bank_each):
-            width = len(GROUPS[g]) * CHUNK
-            if bank_each:
-                banks = [psum.tile([P, 1, width], F32, name="block_bank", tag="bank") for a in range(OUT_BLOCKS)]
-                out_banks[g] = [banks[a][:, 0:1, :] for a in range(OUT_BLOCKS)]
-            else:
-                bank = psum.tile([P, OUT_BLOCKS, width], F32, name="out_bank", tag="bank")
-                out_banks[g] = [bank[:, a : a + 1, :] for a in range(OUT_BLOCKS)] + [bank[:]]
-            for a in range(OUT_BLOCKS):
+        def second_layer(chunks, a):
+            bank = psum.tile([P, len(chunks), CHUNK], F32, name="out_bank", tag="bank")
+            for n, c in enumerate(chunks):
                 nc.tensor.matmul_mx(
-                    out=out_banks[g][a][:, 0, :],
+                    out=bank[:, n, :],
                     lhsT=w2_codes[:, a * 2 * P : (a + 1) * 2 * P].bitcast(FP4X4),
                     lhsT_scale=w2_plane[:, a * P : (a + 1) * P],
-                    rhs=h_codes[g][:].bitcast(FP8X4),
-                    rhs_scale=h_planes[g][:],
+                    rhs=h_codes[c][:].bitcast(FP8X4),
+                    rhs_scale=h_planes[c][:],
                     start=True,
                     stop=True,
                 )
+            out_banks[chunks, a] = bank
 
-        def leave(g, a, on_vector):
-            result = keep.tile([P, 1, UNIT], F32, name=f"result{g}_{a}", **(vector_turn if on_vector else scalar_turn))
+        def both_blocks(chunks):
+            for a in range(OUT_BLOCKS):
+                second_layer(chunks, a)
+
+        def leave(chunks, a, on_vector):
+            result = keep.tile([P, UNIT], F32, name=f"result{chunks[0]}_{a}", **(vector_turn if on_vector else scalar_turn))
+            bank = out_banks[chunks, a][:].rearrange("p c n -> p (c n)")
             if on_vector:
-                nc.vector.tensor_copy(result[:], out_banks[g][a])
+                nc.vector.tensor_copy(result[:], bank)
             else:
-                nc.scalar.copy(result[:], out_banks[g][a])
-            nc.sync.dma_start(out_rows[:, a : a + 1, g * UNIT : (g + 1) * UNIT], result[:])
+                nc.scalar.copy(result[:], bank)
+            nc.sync.dma_start(out_rows[:, a, chunks[0] * CHUNK : (chunks[-1] + 1) * CHUNK], result[:])
 
-        for c in range(CHUNKS - 1):
+        for c in range(6):
             first_layer(c)
-        relu(0, 0)
-        quantise(0, (0,))
-        relu(0, 1)
-        relu(1, 2)
-        quantise(0, (1,))
-        second_layer(0, bank_each=True)
-        first_layer(CHUNKS - 1)
-        relu(1, 3)
-        for g in range(2, 5):
-            for c in GROUPS[g]:
-                relu(g, c)
-        quantise(1, GROUPS[1])
-        second_layer(1, bank_each=True)
-        leave(0, 0, on_vector=True)
-        quantise(2, GROUPS[2])
-        second_layer(2, bank_each=True)
-        leave(0, 1, on_vector=True)
-        leave(1, 0, on_vector=True)
-        leave(1, 1, on_vector=False)
-        for g in (3, 4):
-            quantise(g, GROUPS[g])
-            second_layer(g, bank_each=True)
-        leave(2, 0, on_vector=False)
-        leave(2, 1, on_vector=True)
-        last = keep.tile([P, OUT_BLOCKS, UNIT], F32, name="last", **scalar_turn)
-        for n, g in enumerate((3, 4)):
-            nc.scalar.copy(last[:, 0:1, n * CHUNK : (n + 1) * CHUNK], out_banks[g][0])
-            nc.vector.tensor_copy(last[:, 1:2, n * CHUNK : (n + 1) * CHUNK], out_banks[g][1])
-        nc.sync.dma_start(out_rows[:, :, S - UNIT : S], last[:])
+        for c in range(3):
+            relu(c, on_vector=False)
+        quantise(0)
+        quantise(1)
+        both_blocks((0, 1))
+        first_layer(6)
+        first_layer(7)
+        relu(3, on_vector=True)
+        quantise(2)
+        quantise(3)
+        both_blocks((2, 3))
+        for c in range(4, 7):
+            relu(c, on_vector=False)
+        first_result = keep.tile([P, OUT_BLOCKS, UNIT], F32, name="first_result", **vector_turn)
+        for a in range(OUT_BLOCKS):
+            nc.vector.tensor_copy(first_result[:, a, :], out_banks[(0, 1), a][:].rearrange("p c n -> p (c n)"))
+        nc.sync.dma_start(out_rows[:, :, 0:UNIT], first_result[:])
+        quantise(4)
+        quantise(5)
+        both_blocks((4, 5))
+        relu(7, on_vector=True)
+        leave((2, 3), 0, on_vector=False)
+        leave((2, 3), 1, on_vector=False)
+        for c in (6, 7):
+            quantise(c)
+            both_blocks((c,))
+        leave((4, 5), 0, on_vector=False)
+        leave((4, 5), 1, on_vector=True)
+        for c in (6, 7):
+            result = keep.tile([P, OUT_BLOCKS, CHUNK], F32, name=f"last{c}", **scalar_turn)
+            nc.scalar.copy(result[:, 0, :], out_banks[(c,), 0][:, 0, :])
+            nc.vector.tensor_copy(result[:, 1, :], out_banks[(c,), 1][:, 0, :])
+            nc.sync.dma_start(out_rows[:, :, c * CHUNK : (c + 1) * CHUNK], result[:])

@@ -96,7 +96,7 @@ def tile_picked_phmlp_relu_p_kernel(tc, x_words, x_scales, w1, w2_words, w2_scal
         w2_codes = keep.tile([P, 2 * N], U8, name="w2_codes", **vector_turn)
         nc.sync.dma_start(w2_codes[:].bitcast(I32), w2_words[0].bitcast(I32))
         w2_plane = keep.tile([P, N], U8, name="w2_plane", **vector_turn)
-        nc.vector.memset(w2_plane[:].bitcast(I32), 0)
+        nc.gpsimd.memset(w2_plane[:].bitcast(I32), 0)
         for q in range(P // QUAD):
             w2_rows = w2_scales[0, PACK * q : PACK * (q + 1), :]
             nc.sync.dma_start(w2_plane[QUAD * q : QUAD * q + PACK, :].bitcast(I32), w2_rows.bitcast(I32))
@@ -114,17 +114,16 @@ def tile_picked_phmlp_relu_p_kernel(tc, x_words, x_scales, w1, w2_words, w2_scal
             )
 
         xw_picked = []
-        for u in range(UNITS):
-            words = keep.tile([P, UNIT], U32, name=f"xw_picked{u}", **vector_turn)
-            entries = offsets[:, u * (UNIT // GROUP) : (u + 1) * (UNIT // GROUP)]
+        for first, width in ((0, UNIT), (UNIT, UNIT), (HALF, HALF)):
+            words = keep.tile([P, width], U32, name=f"xw_picked{first}", **vector_turn)
+            entries = offsets[:, first // GROUP : (first + width) // GROUP]
             nc.vector.tensor_copy(words[:], xw_table[:].indirect(entries))
-            xw_picked.append(words)
+            xw_picked.extend(words[:, lo : lo + CHUNK] for lo in range(0, width, CHUNK))
 
         out_rows = out.rearrange("(a p) s -> p a s", p=P)
         h_banks, h_bf, h_codes, h_planes, out_banks = {}, {}, {}, {}, {}
 
         def first_layer(c):
-            u, in_unit = divmod(c, PER_UNIT)
             v, in_half = divmod(c, HALF // CHUNK)
             h_banks[c] = psum.tile([P, PACK, CHUNK], F32, name="h_bank", tag="bank")
             for t in range(PACK):
@@ -132,7 +131,7 @@ def tile_picked_phmlp_relu_p_kernel(tc, x_words, x_scales, w1, w2_words, w2_scal
                     out=h_banks[c][:, t, :],
                     lhsT=w1_codes[:, t * P : (t + 1) * P].bitcast(FP8X4),
                     lhsT_scale=w1_plane[:, t * P : (t + 1) * P],
-                    rhs=xw_picked[u][:, in_unit * CHUNK : (in_unit + 1) * CHUNK].bitcast(FP8X4),
+                    rhs=xw_picked[c].bitcast(FP8X4),
                     rhs_scale=xs_planes[v][:, in_half * CHUNK : (in_half + 1) * CHUNK],
                     start=True,
                     stop=True,
@@ -151,23 +150,23 @@ def tile_picked_phmlp_relu_p_kernel(tc, x_words, x_scales, w1, w2_words, w2_scal
             h_planes[c] = keep.tile([P, CHUNK], U8, name=f"h_plane{c}", align_bytes=64)
             nc.vector.quantize_mx(out=h_codes[c][:].bitcast(FP8X4), scales=h_planes[c][:], in_=h_bf[c][:].rearrange("p n t -> p (n t)"))
 
-        def second_layer(chunks, a):
-            bank = psum.tile([P, len(chunks), CHUNK], F32, name="out_bank", tag="bank")
-            for n, c in enumerate(chunks):
-                nc.tensor.matmul_mx(
-                    out=bank[:, n, :],
-                    lhsT=w2_codes[:, a * 2 * P : (a + 1) * 2 * P].bitcast(FP4X4),
-                    lhsT_scale=w2_plane[:, a * P : (a + 1) * P],
-                    rhs=h_codes[c][:].bitcast(FP8X4),
-                    rhs_scale=h_planes[c][:],
-                    start=True,
-                    stop=True,
-                )
-            out_banks[chunks, a] = bank
+        def second_pass(target, c, a):
+            nc.tensor.matmul_mx(
+                out=target,
+                lhsT=w2_codes[:, a * 2 * P : (a + 1) * 2 * P].bitcast(FP4X4),
+                lhsT_scale=w2_plane[:, a * P : (a + 1) * P],
+                rhs=h_codes[c][:].bitcast(FP8X4),
+                rhs_scale=h_planes[c][:],
+                start=True,
+                stop=True,
+            )
 
         def both_blocks(chunks):
-            for a in range(OUT_BLOCKS):
-                second_layer(chunks, a)
+            for n, c in enumerate(chunks):
+                for a in range(OUT_BLOCKS):
+                    if n == 0:
+                        out_banks[chunks, a] = psum.tile([P, len(chunks), CHUNK], F32, name="out_bank", tag="bank")
+                    second_pass(out_banks[chunks, a][:, n, :], c, a)
 
         def leave(chunks, a, on_vector):
             result = keep.tile([P, UNIT], F32, name=f"result{chunks[0]}_{a}", **(vector_turn if on_vector else scalar_turn))
@@ -184,7 +183,10 @@ def tile_picked_phmlp_relu_p_kernel(tc, x_words, x_scales, w1, w2_words, w2_scal
             relu(c, on_vector=False)
         quantise(0)
         quantise(1)
-        both_blocks((0, 1))
+        first_bank = psum.tile([P, OUT_BLOCKS, PER_UNIT, CHUNK], F32, name="out_bank", tag="bank")
+        for c in range(PER_UNIT):
+            for a in range(OUT_BLOCKS):
+                second_pass(first_bank[:, a, c, :], c, a)
         first_layer(6)
         first_layer(7)
         relu(3, on_vector=True)
@@ -194,8 +196,7 @@ def tile_picked_phmlp_relu_p_kernel(tc, x_words, x_scales, w1, w2_words, w2_scal
         for c in range(4, 7):
             relu(c, on_vector=False)
         first_result = keep.tile([P, OUT_BLOCKS, UNIT], F32, name="first_result", **vector_turn)
-        for a in range(OUT_BLOCKS):
-            nc.vector.tensor_copy(first_result[:, a, :], out_banks[(0, 1), a][:].rearrange("p c n -> p (c n)"))
+        nc.vector.tensor_copy(first_result[:], first_bank[:].rearrange("p a c n -> p a (c n)"))
         nc.sync.dma_start(out_rows[:, :, 0:UNIT], first_result[:])
         quantise(4)
         quantise(5)

@@ -30,6 +30,9 @@ PER_UNIT = UNIT // CHUNK
 OUT_BLOCKS = N // P
 PAIR = 2
 WARM_UP_WIDTHS = (512, 64)
+SPAN = 256
+WEIGHT_SHIFT = 128
+PLANE_SHIFT = 64
 CAST_SPLIT = 96
 
 
@@ -46,9 +49,10 @@ def tile_picked_phmlp_relu_p_kernel(tc, x_words, x_scales, w1, w2_words, w2_scal
 
         xs_table = keep.tile([P, T], U8, name="xs_table", align_bytes=64)
         nc.vector.memset(xs_table[:].bitcast(I32), 0)
-        first_plane = keep.tile([P, HALF], U8, name="xs_plane0", **load_turn)
-        nc.vector.memset(first_plane[:].bitcast(I32), 0)
-        xs_planes = [first_plane, keep.tile([P, HALF], U8, name="xs_plane1", align_bytes=64)]
+        first_plane = keep.tile([P, PLANE_SHIFT + HALF], U8, name="xs_plane0", **load_turn)[:, PLANE_SHIFT:]
+        nc.vector.memset(first_plane.bitcast(I32), 0)
+        second_plane = keep.tile([P, HALF + SPAN], U8, name="xs_plane1", align_bytes=64)[:, PLANE_SHIFT : PLANE_SHIFT + HALF]
+        xs_planes = [first_plane, second_plane]
 
         w1_rows = w1.rearrange("(p j) c -> p j c", j=PACK)
         w1_head = keep.tile([P, 1, H], F32, name="w1_head")
@@ -66,7 +70,7 @@ def tile_picked_phmlp_relu_p_kernel(tc, x_words, x_scales, w1, w2_words, w2_scal
             entries = offsets[:, v * (HALF // GROUP) : (v + 1) * (HALF // GROUP)]
             nc.vector.tensor_copy(xs_picked[:], xs_table[:].indirect(entries))
             if v > 0:
-                nc.vector.tensor_copy(xs_planes[v][:].bitcast(I32), xs_picked[:].bitcast(I32))
+                nc.vector.tensor_copy(xs_planes[v].bitcast(I32), xs_picked[:].bitcast(I32))
             for r in range(min(v, 1), PACK):
                 nc.sync.dma_start(xs_planes[v][r:P:QUAD, :].bitcast(I32), xs_picked[BLOCK_ROWS * r : P : QUAD, :].bitcast(I32))
 
@@ -85,18 +89,19 @@ def tile_picked_phmlp_relu_p_kernel(tc, x_words, x_scales, w1, w2_words, w2_scal
             rest_dst = w1_bf[first_tile][:].rearrange("p t m j -> p m t j")
             cast(rest_dst[:, lo:hi, :, 1:PACK], rest_src[:, lo:hi, first_tile : first_tile + PAIR])
 
-        w1_codes = keep.tile([P, PACK * P], U32, name="w1_codes", align_bytes=64)
-        w1_plane = keep.tile([P, PACK * P], U8, name="w1_plane", **vector_turn)
+        shift = WEIGHT_SHIFT // PACK
+        w1_codes = keep.tile([P, PACK * P + 2 * shift], U32, name="w1_codes", align_bytes=64)[:, shift : shift + PACK * P]
+        w1_plane = keep.tile([P, PLANE_SHIFT + PACK * P], U8, name="w1_plane", **vector_turn)[:, PLANE_SHIFT:]
         for first_tile in (PAIR, 0):
             pair_codes = w1_codes[:, first_tile * P : (first_tile + PAIR) * P]
             pair_plane = w1_plane[:, first_tile * P : (first_tile + PAIR) * P]
             pair_bf = w1_bf[first_tile][:].rearrange("p t m j -> p (t m j)")
             nc.vector.quantize_mx(out=pair_codes.bitcast(FP8X4), scales=pair_plane, in_=pair_bf)
 
-        w2_codes = keep.tile([P, 2 * N], U8, name="w2_codes", **vector_turn)
-        nc.sync.dma_start(w2_codes[:].bitcast(I32), w2_words[0].bitcast(I32))
-        w2_plane = keep.tile([P, N], U8, name="w2_plane", **vector_turn)
-        nc.gpsimd.memset(w2_plane[:].bitcast(I32), 0)
+        w2_codes = keep.tile([P, WEIGHT_SHIFT + 2 * N], U8, name="w2_codes", **vector_turn)[:, WEIGHT_SHIFT:]
+        nc.sync.dma_start(w2_codes.bitcast(I32), w2_words[0].bitcast(I32))
+        w2_plane = keep.tile([P, PLANE_SHIFT + N], U8, name="w2_plane", **vector_turn)[:, PLANE_SHIFT:]
+        nc.gpsimd.memset(w2_plane.bitcast(I32), 0)
         for q in range(P // QUAD):
             w2_rows = w2_scales[0, PACK * q : PACK * (q + 1), :]
             nc.sync.dma_start(w2_plane[QUAD * q : QUAD * q + PACK, :].bitcast(I32), w2_rows.bitcast(I32))
@@ -147,8 +152,8 @@ def tile_picked_phmlp_relu_p_kernel(tc, x_words, x_scales, w1, w2_words, w2_scal
 
         def quantise(c):
             h_codes[c] = keep.tile([P, CHUNK], U32, name=f"h_codes{c}", **vector_turn)
-            h_planes[c] = keep.tile([P, CHUNK], U8, name=f"h_plane{c}", align_bytes=64)
-            nc.vector.quantize_mx(out=h_codes[c][:].bitcast(FP8X4), scales=h_planes[c][:], in_=h_bf[c][:].rearrange("p n t -> p (n t)"))
+            h_planes[c] = keep.tile([P, SPAN], U8, name=f"h_plane{c}", align_bytes=64)[:, PLANE_SHIFT : PLANE_SHIFT + CHUNK]
+            nc.vector.quantize_mx(out=h_codes[c][:].bitcast(FP8X4), scales=h_planes[c], in_=h_bf[c][:].rearrange("p n t -> p (n t)"))
 
         def second_pass(target, c, a):
             nc.tensor.matmul_mx(
@@ -156,7 +161,7 @@ def tile_picked_phmlp_relu_p_kernel(tc, x_words, x_scales, w1, w2_words, w2_scal
                 lhsT=w2_codes[:, a * 2 * P : (a + 1) * 2 * P].bitcast(FP4X4),
                 lhsT_scale=w2_plane[:, a * P : (a + 1) * P],
                 rhs=h_codes[c][:].bitcast(FP8X4),
-                rhs_scale=h_planes[c][:],
+                rhs_scale=h_planes[c],
                 start=True,
                 stop=True,
             )

@@ -29,7 +29,6 @@ HALVES, UNITS, CHUNKS = S // HALF, S // UNIT, S // CHUNK
 PER_UNIT = UNIT // CHUNK
 OUT_BLOCKS = N // P
 PAIR = 2
-WARM_UP_WIDTHS = (512, 64)
 SPAN = 256
 WEIGHT_SHIFT = 128
 PLANE_SHIFT = 64
@@ -105,18 +104,6 @@ def tile_picked_phmlp_relu_p_kernel(tc, x_words, x_scales, w1, w2_words, w2_scal
         for q in range(P // QUAD):
             w2_rows = w2_scales[0, PACK * q : PACK * (q + 1), :]
             nc.sync.dma_start(w2_plane[QUAD * q : QUAD * q + PACK, :].bitcast(I32), w2_rows.bitcast(I32))
-
-        warm_bank = psum.tile([P, H], F32, name="warm_bank", tag="bank")
-        for width in WARM_UP_WIDTHS:
-            nc.tensor.matmul_mx(
-                out=warm_bank[:, 0:width],
-                lhsT=w1_codes[:, 0:P].bitcast(FP8X4),
-                lhsT_scale=w1_plane[:, 0:P],
-                rhs=w1_codes[:, 0:width].bitcast(FP8X4),
-                rhs_scale=w1_plane[:, 0:width],
-                start=True,
-                stop=True,
-            )
 
         xw_picked = []
         for first, width in ((0, UNIT), (UNIT, UNIT), (HALF, HALF)):

from contextlib import ExitStack

import concourse.mybir as mybir

K, T, S, H, N = 512, 2048, 1024, 512, 256
FLOPS = 2 * K * H * S + 2 * H * N * S

F32 = mybir.dt.float32
BF16 = mybir.dt.bfloat16
I32 = mybir.dt.int32
U32 = mybir.dt.uint32
U16 = mybir.dt.uint16
U8 = mybir.dt.uint8
FP8X4 = mybir.dt.float8_e4m3fn_x4
FP4X4 = mybir.dt.float4_e2m1fn_x4
RELU = mybir.ActivationFunctionType.Relu

P = 128
PACK = 4
QUAD = 32
GROUP = 16
BLOCK_ROWS = 8
BANKS = 8

HALF = 512
UNIT = 256
CHUNK = 128
HALVES, UNITS, CHUNKS = S // HALF, S // UNIT, S // CHUNK
PER_UNIT = UNIT // CHUNK
OUT_BLOCKS = N // P
PAIR = 2
SPAN = 256
WEIGHT_SHIFT = 128
PLANE_SHIFT = 64
CAST_SPLIT = 96


def tile_picked_phmlp_relu_p_kernel(tc, x_words, x_scales, w1, w2_words, w2_scales, offs, out):
    nc = tc.nc
    with ExitStack() as ctx:
        keep = ctx.enter_context(tc.tile_pool(name="keep", bufs=1))
        psum = ctx.enter_context(tc.psum_pool(name="psum", bufs=BANKS))

        load_turn = dict(tag="load_turn", bufs=1 + 2, align_bytes=64)
        vector_slots = 26
        scalar_turn = dict(tag="scalar_turn", bufs=11, align_bytes=64)
        vector_turn = dict(tag="vector_turn", bufs=vector_slots, align_bytes=64)

        xs_table = keep.tile([P, T], U8, name="xs_table", align_bytes=64)
        nc.vector.memset(xs_table[:].bitcast(I32), 0)
        first_plane = keep.tile([P, PLANE_SHIFT + HALF], U8, name="xs_plane0", **load_turn)[:, PLANE_SHIFT:]
        nc.vector.memset(first_plane.bitcast(I32), 0)
        second_plane = keep.tile([P, HALF + SPAN], U8, name="xs_plane1", align_bytes=64)[:, PLANE_SHIFT : PLANE_SHIFT + HALF]
        xs_planes = [first_plane, second_plane]

        w1_rows = w1.rearrange("(p j) c -> p j c", j=PACK)
        w1_head = keep.tile([P, 1, H], F32, name="w1_head")
        nc.sync.dma_start(w1_head[:], w1_rows[:, 0:1, :])
        offsets = keep.tile([P, S // GROUP], U16, name="offsets")
        nc.sync.dma_start(offsets[:], offs)
        nc.sync.dma_start(xs_table[0:P:BLOCK_ROWS, :].bitcast(I32), x_scales[0].bitcast(I32))
        w1_rest = keep.tile([P, PACK - 1, H], F32, name="w1_rest", **load_turn)
        nc.sync.dma_start(w1_rest[:], w1_rows[:, 1:PACK, :])
        xw_table = keep.tile([P, T], U32, name="xw_table", **load_turn)
        nc.sync.dma_start(xw_table[:].bitcast(I32), x_words[0].rearrange("p n t -> p (n t)").bitcast(I32))

        for v in range(HALVES):
            xs_picked = keep.tile([P, HALF], U8, name=f"xs_picked{v}", **vector_turn)
            entries = offsets[:, v * (HALF // GROUP) : (v + 1) * (HALF // GROUP)]
            nc.vector.tensor_copy(xs_picked[:], xs_table[:].indirect(entries))
            if v > 0:
                nc.vector.tensor_copy(xs_planes[v].bitcast(I32), xs_picked[:].bitcast(I32))
            for r in range(min(v, 1), PACK):
                nc.sync.dma_start(xs_planes[v][r:P:QUAD, :].bitcast(I32), xs_picked[BLOCK_ROWS * r : P : QUAD, :].bitcast(I32))

        w1_bf = {first_tile: keep.tile([P, PAIR, P, PACK], BF16, name=f"w1_bf{first_tile}", align_bytes=64) for first_tile in (PAIR, 0)}
        head_src = w1_head[:, 0, :].rearrange("p (n e t) -> p n t e", e=2, t=PACK)
        rest_src = w1_rest[:].rearrange("p j (m t) -> p m t j", t=PACK)
        shares = (
            (nc.scalar.copy, PAIR, 0, P),
            (nc.vector.tensor_copy, 0, 0, CAST_SPLIT),
            (nc.scalar.copy, 0, CAST_SPLIT, P),
        )
        for cast, first_tile, lo, hi in shares:
            head_dst = w1_bf[first_tile][:, :, :, 0].rearrange("p t (n e) -> p n t e", e=2)
            cast(head_dst[:, lo // 2 : hi // 2], head_src[:, lo // 2 : hi // 2, first_tile : first_tile + PAIR])
        for cast, first_tile, lo, hi in shares:
            rest_dst = w1_bf[first_tile][:].rearrange("p t m j -> p m t j")
            cast(rest_dst[:, lo:hi, :, 1:PACK], rest_src[:, lo:hi, first_tile : first_tile + PAIR])

        shift = WEIGHT_SHIFT // PACK
        w1_codes = keep.tile([P, PACK * P + 2 * shift], U32, name="w1_codes", align_bytes=64)[:, shift : shift + PACK * P]
        w1_plane = keep.tile([P, PLANE_SHIFT + PACK * P], U8, name="w1_plane", **vector_turn)[:, PLANE_SHIFT:]
        for first_tile in (PAIR, 0):
            pair_codes = w1_codes[:, first_tile * P : (first_tile + PAIR) * P]
            pair_plane = w1_plane[:, first_tile * P : (first_tile + PAIR) * P]
            pair_bf = w1_bf[first_tile][:].rearrange("p t m j -> p (t m j)")
            nc.vector.quantize_mx(out=pair_codes.bitcast(FP8X4), scales=pair_plane, in_=pair_bf)

        w2_codes = keep.tile([P, WEIGHT_SHIFT + 2 * N], U8, name="w2_codes", **vector_turn)[:, WEIGHT_SHIFT:]
        nc.sync.dma_start(w2_codes.bitcast(I32), w2_words[0].bitcast(I32))
        w2_plane = keep.tile([P, PLANE_SHIFT + N], U8, name="w2_plane", **vector_turn)[:, PLANE_SHIFT:]
        nc.gpsimd.memset(w2_plane.bitcast(I32), 0)
        for q in range(P // QUAD):
            w2_rows = w2_scales[0, PACK * q : PACK * (q + 1), :]
            nc.sync.dma_start(w2_plane[QUAD * q : QUAD * q + PACK, :].bitcast(I32), w2_rows.bitcast(I32))

        xw_picked = []
        for first, width in ((0, UNIT), (UNIT, UNIT), (HALF, HALF)):
            words = keep.tile([P, width], U32, name=f"xw_picked{first}", **vector_turn)
            entries = offsets[:, first // GROUP : (first + width) // GROUP]
            nc.vector.tensor_copy(words[:], xw_table[:].indirect(entries))
            xw_picked.extend(words[:, lo : lo + CHUNK] for lo in range(0, width, CHUNK))

        out_rows = out.rearrange("(a p) s -> p a s", p=P)
        h_banks, h_bf, h_codes, h_planes, out_banks = {}, {}, {}, {}, {}

        def first_layer(c):
            v, in_half = divmod(c, HALF // CHUNK)
            h_banks[c] = psum.tile([P, PACK, CHUNK], F32, name="h_bank", tag="bank")
            for t in range(PACK):
                nc.tensor.matmul_mx(
                    out=h_banks[c][:, t, :],
                    lhsT=w1_codes[:, t * P : (t + 1) * P].bitcast(FP8X4),
                    lhsT_scale=w1_plane[:, t * P : (t + 1) * P],
                    rhs=xw_picked[c].bitcast(FP8X4),
                    rhs_scale=xs_planes[v][:, in_half * CHUNK : (in_half + 1) * CHUNK],
                    start=True,
                    stop=True,
                )

        def relu(c, on_vector):
            h_bf[c] = keep.tile([P, CHUNK, PACK], BF16, name=f"h_bf{c}", **(vector_turn if on_vector else scalar_turn))
            h_src = h_banks[c][:].rearrange("p t n -> p n t")
            if on_vector:
                nc.vector.tensor_scalar_max(h_bf[c][:], h_src, 0.0)
            else:
                nc.scalar.activation(h_bf[c][:], h_src, RELU)

        def quantise(c):
            h_codes[c] = keep.tile([P, CHUNK], U32, name=f"h_codes{c}", **vector_turn)
            h_planes[c] = keep.tile([P, SPAN], U8, name=f"h_plane{c}", align_bytes=64)[:, PLANE_SHIFT : PLANE_SHIFT + CHUNK]
            nc.vector.quantize_mx(out=h_codes[c][:].bitcast(FP8X4), scales=h_planes[c], in_=h_bf[c][:].rearrange("p n t -> p (n t)"))

        def second_pass(target, c, a):
            nc.tensor.matmul_mx(
                out=target,
                lhsT=w2_codes[:, a * 2 * P : (a + 1) * 2 * P].bitcast(FP4X4),
                lhsT_scale=w2_plane[:, a * P : (a + 1) * P],
                rhs=h_codes[c][:].bitcast(FP8X4),
                rhs_scale=h_planes[c],
                start=True,
                stop=True,
            )

        def both_blocks(chunks):
            for n, c in enumerate(chunks):
                for a in range(OUT_BLOCKS):
                    if n == 0:
                        out_banks[chunks, a] = psum.tile([P, len(chunks), CHUNK], F32, name="out_bank", tag="bank")
                    second_pass(out_banks[chunks, a][:, n, :], c, a)

        def leave(chunks, a, on_vector):
            result = keep.tile([P, UNIT], F32, name=f"result{chunks[0]}_{a}", **(vector_turn if on_vector else scalar_turn))
            bank = out_banks[chunks, a][:].rearrange("p c n -> p (c n)")
            if on_vector:
                nc.vector.tensor_copy(result[:], bank)
            else:
                nc.scalar.copy(result[:], bank)
            nc.sync.dma_start(out_rows[:, a, chunks[0] * CHUNK : (chunks[-1] + 1) * CHUNK], result[:])

        for c in range(6):
            first_layer(c)
        for c in range(3):
            relu(c, on_vector=False)
        quantise(0)
        quantise(1)
        first_bank = psum.tile([P, OUT_BLOCKS, PER_UNIT, CHUNK], F32, name="out_bank", tag="bank")
        for c in range(PER_UNIT):
            for a in range(OUT_BLOCKS):
                second_pass(first_bank[:, a, c, :], c, a)
        first_layer(6)
        first_layer(7)
        relu(3, on_vector=True)
        quantise(2)
        quantise(3)
        both_blocks((2, 3))
        for c in range(4, 7):
            relu(c, on_vector=False)
        first_result = keep.tile([P, OUT_BLOCKS, UNIT], F32, name="first_result", **vector_turn)
        nc.vector.tensor_copy(first_result[:], first_bank[:].rearrange("p a c n -> p a (c n)"))
        nc.sync.dma_start(out_rows[:, :, 0:UNIT], first_result[:])
        quantise(4)
        quantise(5)
        both_blocks((4, 5))
        relu(7, on_vector=True)
        leave((2, 3), 0, on_vector=False)
        leave((2, 3), 1, on_vector=False)
        for c in (6, 7):
            quantise(c)
            both_blocks((c,))
        leave((4, 5), 0, on_vector=False)
        leave((4, 5), 1, on_vector=True)
        for c in (6, 7):
            result = keep.tile([P, OUT_BLOCKS, CHUNK], F32, name=f"last{c}", **scalar_turn)
            nc.scalar.copy(result[:, 0, :], out_banks[(c,), 0][:, 0, :])
            nc.vector.tensor_copy(result[:, 1, :], out_banks[(c,), 1][:, 0, :])
            nc.sync.dma_start(out_rows[:, :, c * CHUNK : (c + 1) * CHUNK], result[:])
